import numpy as np, ml_dtypes
CORES = [16,18,20,22]
N = 4
import mx_ref
BF = ml_dtypes.bfloat16
def cols(t, e):
    v = np.concatenate([t.reshape(128, -1, 4), np.zeros((128, 1, 4), BF)], axis=1)
    return np.ascontiguousarray(v[:, e]).reshape(128, -1)
def cut(t, i, w=512):
    return t[:, w * i:w * i + w]
def f(rng, *shape):
    return mx_ref.flush((rng.standard_normal(shape, dtype=np.float32) * np.exp2(rng.integers(-2, 3, shape[:-1] + (1,)))).astype(BF))
def wide(rng, *shape, cols=0):
    v = rng.standard_normal(shape, dtype=np.float32) * np.exp2(rng.integers(-12, 13, shape)).astype(np.float32)
    if cols: v *= np.repeat(np.exp2(rng.integers(-cols, cols + 1, shape[:-2] + (1, shape[-1] // 4))) * (rng.random(shape[:-2] + (1, shape[-1] // 4)) > 0.0625), 4, axis=-1).astype(np.float32)
    return mx_ref.flush(v.astype(BF))
WD, T, PL, CP, NC = 16, 256, 128, 32, 112
def scores(u, x):
    return np.stack([mx_ref.matmul(mx_ref.quantize(u[r]), mx_ref.quantize(x[r]))[0] for r in range(N)])
def fronts(P):
    a = np.zeros(P.shape, bool)
    v, h = P[1:] != P[:-1], P[:, 1:] != P[:, :-1]
    a[1:] |= v; a[:-1] |= v; a[:, 1:] |= h; a[:, :-1] |= h
    return a
def dealt(P):
    i, j = np.nonzero(fronts(P))
    g = np.full((16 * N + 2, WD + 2), -1)
    g[1:-1, 1:-1] = np.arange(N * T).reshape(16 * N, WD)
    n = np.arange(len(i)); D = np.full((N, PL, 5), -1)
    D[(n // 8) % N, 8 * (n // (8 * N)) + n % 8] = np.stack([g[i + 1, j + 1], g[i, j + 1], g[i + 2, j + 1], g[i + 1, j], g[i + 1, j + 2]], axis=1)
    return D
def needed(P):
    return np.stack([np.bincount(e[e >= 0] // T, minlength=N) for e in [np.unique(k) for k in dealt(P)]])
def broken(P):
    if np.sum(fronts(P)) > PL * N: return ["too many active cells"]
    b = []; D = dealt(P)
    for r in range(N):
        c, e = D[r, :, 0], np.unique(D[r])
        if np.bincount(c[c >= 0] // T, minlength=N).max() > CP: b.append("cells of one stripe dealt to one rank")
        if np.bincount(e[e >= 0] // T, minlength=N).max() > NC: b.append("columns of one stripe that one rank needs")
    return b
def smooth(rng, i):
    a, b = np.indices((16 * N, WD)); g = 0
    for _ in range(6):
        t, k, p = rng.uniform(-1, 1), 0.7 * 0.97 ** i * rng.uniform(0.7, 1.4), rng.uniform(0, 6.2832)
        g = g + np.cos(k * (np.cos(t) * a + np.sin(t) * b) + p)
    return g > 0
def straight(rng, i):
    a = np.indices((16 * N, WD))[0]
    return ((a + rng.integers(1, 4)) // 4) % 2 == 0
def islands(rng, i):
    at = [(0, 0), (15, WD // 2)]
    for c in rng.permutation(N * T):
        if len(at) >= int(N * T * 0.0625 * 0.98 ** i): break
        p, q = divmod(int(c), WD)
        if all(abs(p - a) + abs(q - b) >= 3 for a, b in at): at.append((p, q))
    P = np.zeros((16 * N, WD), bool)
    for p, q in at: P[p, q] = True
    return P
def few(rng, i):
    gone = [int(q) for q in 1 + rng.permutation(N - 1)[:rng.integers(1, 3)]]
    if len(gone) == 2 and abs(gone[0] - gone[1]) == 1: gone.pop()
    here = [q for q in range(N) if q not in gone]
    free = [q for q in here if q - 1 not in gone and q + 1 not in gone]
    P = np.zeros((16 * N, WD), bool)
    for q in here:
        if q - 1 in gone: P[16 * q + 1, rng.integers(0, WD)] = True
        if q + 1 in gone: P[16 * q + 14, rng.integers(0, WD)] = True
    for q in free + here[:rng.integers(0, 2)]: P[16 * q + rng.integers(1, 16 if q + 1 in here else 15), rng.integers(0, WD)] = True
    return P
def heavy(rng, i):
    a, b = np.indices((16 * N, WD)); n = np.zeros(a.shape, int); most = rng.integers(0, N)
    low = b % 2 == 1 if WD == 8 else ((b % 2 == 0) & (b > 0)) | (b == WD - 1)
    for r in range(N):
        if r == most:
            for k in (6, 10): n += a >= 16 * r + k + low
            n += a >= 16 * r + 14
            if WD == 8: n[16 * r + 2, 0] += 1
            else: n += a >= 16 * r + 2
        else:
            w = rng.integers(5, 12) + max(0, 3 - 0.1 * i) * np.sin(rng.uniform(0.2, 0.8) * np.arange(WD) + rng.uniform(0, 6.2832))
            n += a >= 16 * r + np.clip(np.rint(w), 2, 14)[None, :]
    return n % 2 == 0
def borders(rng, i):
    a, b = np.indices((16 * N, WD))
    return (a // 16 + (b < rng.integers(1, WD))) % 2 == 0
def drawn(rng, make, uneven=False, idle=False):
    for i in range(50):
        P = make(rng, i) ^ bool(rng.integers(0, 2))
        c = fronts(P).reshape(N, T).sum(axis=1)
        if c.sum() < (1 if idle else 8 * N) or broken(P): continue
        m = needed(P) * (1 - np.eye(N, dtype=int))
        if uneven and (c.max() < 3 * c.min() or m.max() != NC): continue
        if idle and not 1 <= (c == 0).sum() <= 2: continue
        if idle and (c.sum() > 8 * (N - 1) or (c.sum() - 1) % 8 < 3): continue
        if idle and not (m.sum(axis=0)[c == 0] > 0).all(): continue
        return P
    raise RuntimeError("no field in 50 tries")
def sized(t):
    v = t.astype(np.float32)
    return np.where(np.abs(v) < 2.0 ** -30, np.float32(0), v).astype(BF)
def plant(rng, P, spread=False):
    u = sized(f(rng, 128, 512)); qu = mx_ref.quantize(u)
    x = np.zeros((N, 128, T, 4), BF); want = P.reshape(N, T)
    for r in range(N):
        left = np.arange(T)
        for i in range(50):
            k = len(left); m = 8 * -(-k // 8)
            t = sized(wide(rng, 128, 4 * m, cols=2) if spread else f(rng, 128, 4 * m))
            s = mx_ref.matmul(qu, mx_ref.quantize(t))[0][:k]
            turn = np.where((s > 0) == want[r, left], 1, -1)
            t = (t.astype(np.float32).reshape(128, m, 4)[:, :k] * turn[None, :, None]).astype(BF)
            ok = np.abs(s) > 32
            x[r][:, left[ok]] = t[:, ok]
            left = left[~ok]
            if len(left) == 0: break
        else: raise RuntimeError("scores too small in 50 tries")
    return {"x": x.reshape(N, 128, 4 * T), "u": np.stack([u] * N), "w": sized(f(rng, N, 128, 5120))}
def setup_inputs(rng):
    return plant(rng, drawn(rng, smooth))
def setup_inputs_few(rng):
    return plant(rng, drawn(rng, few, idle=True))
def setup_inputs_near(rng):
    for i in range(50):
        d = plant(rng, drawn(rng, borders))
        s = scores(d["u"], d["x"])
        e = 1 + int(np.floor(np.log2(float(np.abs(s).min()))))
        d["u"] = sized((d["u"].astype(np.float32) * np.float32(2.0 ** -e)).astype(BF))
        t = scores(d["u"], d["x"])
        if 0.5 < np.abs(t).min() <= 1 and np.array_equal(t > 0, s > 0): return d
    raise RuntimeError("no scores near 0.5 in 50 tries")
def setup_inputs_spread(rng):
    return plant(rng, drawn(rng, islands), spread=True)
def setup_inputs_straight(rng):
    return plant(rng, drawn(rng, straight))
def setup_inputs_uneven(rng):
    return plant(rng, drawn(rng, heavy, uneven=True))
def check_inputs(d):
    b = []
    for k in ("x", "u", "w"):
        v = np.abs(d[k].astype(np.float32))
        if not ((v == 0) | ((v >= 2.0 ** -30) & (v <= 2.0 ** 30))).all(): b.append("sizes of " + k)
    if b: return b
    for r in range(N):
        if not np.array_equal(d["u"][r].astype(np.float32), d["u"][0].astype(np.float32)): b.append("u")
    s = scores(d["u"], d["x"])
    if not (np.abs(s) > 0.5).all(): b.append("score")
    return b + broken((s > 0).reshape(16 * N, WD))
def reference(x, u, w):
    P = (scores(u, x) > 0).reshape(16 * N, WD)
    D = dealt(P)
    m = max(8, 8 * -(-int(np.sum(fronts(P))) // (8 * N)))
    X = np.concatenate(list(x), axis=1)
    y = np.zeros((N, 128, 2 * PL), np.float32)
    for r in range(N):
        for k in range(5):
            q = mx_ref.quantize(cols(X, D[r, :m, k]))
            for o in range(2): y[r][:, PL * o:PL * o + m] += mx_ref.matmul(mx_ref.quantize(cut(w[r], 2 * k + o)), q)
    return {"y": y}

@@ -1,0 +1,346 @@
+from concourse.bass import DstId, RemoteDMATransfer
+from concourse.mybir import dt, AluOpType, ActivationFunctionType
+
+A = AluOpType
+F = ActivationFunctionType
+CODE = "float8_e4m3fn_x4"
+RG = 176
+U = 1.0 / 128
+
+
+def sb(n, d="float32"): return ("sbuf", [128, n], d)
+
+
+BF, I32, U16 = "bfloat16", "int32", "uint16"
+SCRATCH = {
+    "ut": sb(512, BF), "xt": sb(1024, BF), "wt": sb(5120, BF), "zt": sb(640, BF), "xp": sb(1216, BF),
+    "uq": sb(128, CODE), "us": sb(128, "uint8"), "urq": sb(128, CODE), "urs": sb(128, "uint8"),
+    "xq": sb(256, CODE), "xs": sb(256, "uint8"), "padq": sb(544, CODE), "pads": sb(544, "uint8"),
+    "wq": sb(1280, CODE), "ws": sb(1280, "uint8"),
+    "eq": sb(4 * RG + 160, CODE), "es": sb(4 * RG + 160, "uint8"),
+    "xfq": sb(640, CODE), "xfs": sb(640, "uint8"),
+    "off0": sb(8, U16), "ys": sb(256),
+    "sc": ("psum", [128, 1024], "float32"), "yp": ("psum", [128, 1024], "float32"),
+    "pI": sb(1, I32), "pm": sb(4, I32), "pf": sb(4), "i64": sb(8), "i16": sb(8), "kk": sb(8), "kv": sb(8),
+    "b2": sb(1), "b3": sb(1), "nb3": sb(1), "nb2": sb(1), "b7": sb(1), "p16": sb(1), "x8": sb(1),
+    "tp": sb(2), "tp5": sb(2), "te": sb(1), "nP": sb(8), "slot": sb(8), "cE": sb(8), "half": sb(256, BF), "zb": sb(288, BF),
+    "B": sb(64, BF), "BT": sb(64, BF), "EL": sb(64, BF), "eb": sb(64, BF),
+    "P": sb(256, BF), "n2": sb(256, BF), "hp": sb(288, BF), "vp": sb(256, BF), "vn": sb(272, BF), "m1": sb(256, BF), "gh": sb(256, BF),
+    "v2": sb(256, BF), "o2": sb(256, BF), "l": sb(256, BF), "S": sb(288, BF), "FT": sb(32, BF), "RB": sb(32, BF), "R16": sb(32, BF), "Sl": sb(16, BF),
+    "bd": sb(16, BF), "inf": sb(32, BF), "r0": sb(32, BF), "fl": sb(8, BF),
+    "D": sb(2), "D0": sb(2), "D5": sb(2), "K": sb(2, I32), "tb": sb(2), "E1": sb(1), "E5": sb(1), "De": sb(1), "Ke": sb(1, I32), "tbe": sb(1),
+    "junk": sb(288, BF), "junk2": sb(288, BF), "junk3": sb(288, BF), "junk4": sb(16, BF), "acl": sb(2), "ace": sb(1), "iof": sb(12),
+    "en": sb(6), "g": sb(48), "gac": sb(16), "gb": sb(8), "gs": sb(8), "b1": sb(8), "bb": sb(8), "uu": sb(8), "bf": sb(16),
+    "fo": sb(16, U16), "ioo": sb(12, U16), "spo": sb(12),
+}
+for _i in range(3):
+    SCRATCH["of%d" % _i] = sb(12, U16)
+    SCRATCH["sp%d" % _i] = sb(12)
+    SCRATCH["pkq%d" % _i] = sb(RG, CODE)
+    SCRATCH["pks%d" % _i] = sb(RG, "uint8")
+SEMAPHORES = ["vc", "ac", "tc", "pc", "ldu", "ldxa", "ldxb", "ldw0", "ldw1", "ldw2", "ldw3", "ldw4", "halo", "bdr", "inf0", "inf1", "inf2", "inf3",
+              "r0s", "flg", "cq0", "cq1", "cq2", "cs0", "cs1", "cs2", "sent", "st0", "st1"]
+
+
+def rank_program(g, core, T, topo):
+    r = T.rank_of(core)
+    if r is None:
+        return
+    N = len(T.cores)
+    others = [q for q in range(N) if q != r]
+    Q = {"v": g.vector, "a": g.scalar, "t": g.tensor, "p": g, "s": g.sync}
+    cnt, seen = {"sent": 0}, {}
+
+    def wait(qn, deps):
+        for d in deps:
+            if d is not None and seen.get((qn, d[0]), 0) < d[1]:
+                Q[qn].wait_ge(T.sem[d[0]], d[1])
+                seen[(qn, d[0])] = d[1]
+
+    def tok(sem, inst, n):
+        inst.then_inc(T.sem[sem], n)
+        cnt[sem] = cnt.get(sem, 0) + n
+        return (sem, cnt[sem])
+
+    def op(qn, name, deps, *args):
+        wait(qn, deps)
+        q = Q[qn]
+        if name == "memset": i = q.memset(*args)
+        elif name == "tt": i = q.tensor_tensor(*args)
+        elif name == "ts": i = q.tensor_scalar(*args)
+        elif name == "copy": i = q.tensor_copy(*args)
+        elif name == "scan": i = q.tensor_tensor_scan(*args)
+        elif name == "turn": i = q.transpose(*args)
+        elif name == "quant": i = q.quantize_mx(*args)
+        elif name == "act": i = q.activation(*args)
+        elif name == "lin": i = q.activation(args[0], args[1], F.Identity, bias=args[3], scale=args[2])
+        elif name == "sign": i = q.activation(args[0], args[1], F.Sign, bias=args[3], scale=args[2])
+        elif name == "sum": i = q.activation(args[0], args[1], F.Sign, bias=args[3], scale=args[2], accum_out=args[4])
+        elif name == "mm": i = q.matmul_mx(*args)
+        elif name == "iota": i = q.iota(*args)
+        else: i = q.iota(*args, allow_small_or_imprecise_dtypes=True)
+        return tok(qn + "c", i, 1)
+
+    def V(name, deps, *args): return op("v", name, deps, *args)
+    def S(name, deps, *args): return op("a", name, deps, *args)
+
+    def dma(qn, sem, deps, out, in_):
+        wait(qn, deps)
+        return tok(sem, Q[qn].dma_start(out, in_), 16)
+
+    def U8(v): return v.bitcast(dt.uint8)
+    def U32(v): return v.bitcast(dt.uint32)
+    def bits(en): return sum(1 << e for e in en)
+
+    def dest(q):
+        rid, pid, _ = topo.addr(T.cores[q])
+        return DstId(rid=rid, pnc=pid)
+
+    def send(trs):
+        g.remote_dma_fused([RemoteDMATransfer(dst_ids=[dest(q) for q in qs], dma_engine_mask=bits(en), remote_sem=sem, srcs=[src], dsts=dsts)
+                            for qs, en, sem, src, dsts in trs], local_sem=T.sem.sent)
+        cnt["sent"] += sum(len(t[1]) for t in trs)
+
+    def at(q, me): return q if q < me else q - 1
+    eng = {q: topo.engines(core, T.cores[q]) for q in others}
+    ne = min(len(eng[q]) for q in others)
+    e0 = eng[others[0]]
+    h2 = ne // 2
+
+    up, dn = r > 0, r < N - 1
+    ex_out, ex_in = r in (0, 1), r in (1, 2)
+    PB = 128 if dn else 129
+    L = 288 if r == 0 else 272
+    ldu = dma("a", "ldu", [], T.ut[:, 0:8], T.u[:, 0:8])
+    h0, h1 = (0, 1) if up else (1, 0)
+    X = lambda h: slice(512 * h, 512 * h + 512)
+    ldxa = dma("s", "ldxa", [], T.xt[:, X(h0)], T.x[:, X(h0)])
+    ldxb = dma("a", "ldxb", [], T.xt[:, X(h1)], T.x[:, X(h1)])
+    kp = op("p", "iota", [], T.pI[:], [[0, 1]], 0, 1)
+    op("p", "iotaf", [], T.i64[:], [[64, 8]], 0, 0)
+    op("p", "iotaf", [], T.i16[:], [[0, 4], [16, 2]], 0, 0)
+    op("p", "iotaf", [], T.kk[:, 0:3], [[-2, 3]], -2 * (PB - 1) - L, 0)
+    op("p", "iotaf", [], T.kk[:, 3:5], [[-68, 2]], -2 * (PB - 17) - L, 0)
+    op("p", "iotaf", [], T.kv[:, 0:3], [[1, 3]], PB - 1 + 128, 0)
+    kg = op("p", "iotaf", [], T.kv[:, 3:5], [[34, 2]], PB - 17 + 128, 0)
+    mu = V("memset", [], T.ut[:, 8:512], 0.0)
+    mo = V("memset", [], T.off0[:], 0)
+    V("ts", [kp], T.pm[:, 3:4], T.pI[:], 5, None, A.logical_shift_right)
+    V("ts", [], T.pm[:, 0:1], T.pI[:], 15, None, A.bitwise_and)
+    V("ts", [], T.pm[:, 1:2], T.pI[:], 7, None, A.bitwise_and)
+    k = V("ts", [], T.pm[:, 2:3], T.pI[:], 3, 1, A.logical_shift_right, A.bitwise_and)
+    mB = V("memset", [], T.B[:], 0.0)
+    kf = V("copy", [k], T.pf[:], T.pm[:])
+    mz = V("memset", [], T.zt[:], 0.0)
+
+    qu = V("quant", [ldu, mu], T.uq[:], T.us[:], T.ut[:])
+    pu = V("copy", [qu, mo], U32(T.urq[:]), U32(T.uq[:]).indirect(T.off0[:]))
+    pv = S("act", [qu, mo], T.urs[:], T.us[:].indirect(T.off0[:]), F.Copy)
+    qx, mm = {}, {}
+
+    def score(h, ld):
+        c = slice(128 * h, 128 * h + 128)
+        qx[h] = V("quant", [ld], T.xq[:, c], T.xs[:, c], T.xt[:, X(h)])
+        mm[h] = op("t", "mm", [pu, pv, qx[h]], T.sc[:, 512 * h:512 * h + 128], T.urq[:], T.urs[:], T.xq[:, c], T.xs[:, c], True, True)
+    score(h0, ldxa)
+    V("memset", [], T.half[:], 0.5)
+    V("memset", [], T.vn[:, 0:16], -3.0)
+    V("memset", [], T.vn[:, 256:272], -3.0)
+    kz = V("memset", [], T.zb[:], 0.0)
+    score(h1, ldxb)
+    ldw, qw = {}, {}
+
+    def load_w(k, deps): ldw[k] = dma("s", "ldw%d" % k, deps, T.wt[:, 1024 * k:1024 * k + 1024], T.w[:, 1024 * k:1024 * k + 1024])
+    def quant_w(k): qw[k] = V("quant", [ldw[k]], T.wq[:, 256 * k:256 * k + 256], T.ws[:, 256 * k:256 * k + 256], T.wt[:, 1024 * k:1024 * k + 1024])
+    load_w(4, [ldxb])
+
+    nb = ([(r - 1, 0, 400)] if up else []) + ([(r + 1, 240, 112)] if r == N - 2 else [])
+
+    def strips(view, nb):
+        if nb:
+            send([([q], eng[q][(src > 0) * h2:(src > 0) * h2 + h2], T.sem.halo, view("xq", "xs", src), [view("padq", "pads", dst)]) for q, src, dst in nb])
+    for b in nb:
+        wait("p", [qx[b[1] > 0]])
+        strips(lambda q, s, a: U8(T[q][:, a:a + 16]), [b])
+    hal = ("halo", 2 * h2)
+
+    S("lin", [kf, kg], T.b2[:], T.pf[:, 2:3], 32.0, T.pf[:, 1:2])
+    k = S("lin", [], T.p16[:], T.pf[:, 0:1], 2.0 / RG, 4 + 0.5 / RG)
+    k = S("lin", [k], T.b3[:], T.pf[:, 3:4], 8.0, T.b2[:])
+    k = S("lin", [k], T.nb3[:], T.b3[:], -U, -0.5 * U)
+    S("lin", [], T.x8[:], T.pf[:, 2:3], -8.0 / RG, 64.0 / RG)
+    k = S("lin", [k], T.tp[:], T.i64[:, 0:2], -U, T.nb3[:])
+    S("lin", [], T.b7[:], T.pf[:, 3:4], 8.0, T.pf[:, 1:2])
+    k = S("lin", [k], T.tp5[:], T.tp[:], 1.0, 0.5)
+    S("lin", [], T.nb2[:], T.b2[:], U, 8.0 * r * U)
+    S("lin", [k], T.te[:], T.b7[:], -1.0 / 32, -0.5 / 32)
+    k = S("lin", [], T.slot[:], T.i16[:], 2.0 / RG, T.p16[:])
+    S("lin", [k], T.nP[:], T.i64[:], U, T.nb2[:])
+    kS = S("lin", [], T.cE[:], T.i16[:], -1.0 / RG, T.x8[:])
+    xp0 = 128 if dn else 4
+    for i in range(16): kX = S("act", [ldxa, ldxb], T.xp[:, xp0 + 68 * i:xp0 + 68 * i + 64], T.xt[:, 64 * i:64 * i + 64], F.Copy)
+
+    if up: kb = V("ts", [mm[0], mB], T.B[:, 32:48], T.sc[:, 0:16], 0.0, None, A.is_gt)
+    if dn: kb = V("ts", [mm[1], mB], T.B[:, 0:16], T.sc[:, 624:640], 0.0, None, A.is_gt)
+    kb = V("turn", [kb], T.BT[:], T.B[:])
+    for h in (h0, h1): p = V("ts", [mm[h]], T.P[:, 128 * h:128 * h + 128], T.sc[:, 512 * h:512 * h + 128], 0.0, None, A.is_gt)
+    wait("p", [kb])
+    send(([([r - 1], eng[r - 1][:h2], T.sem.bdr, T.BT[:, 32:33], [T.bd[:, 8:9]])] if up else [])
+         + ([([r + 1], eng[r + 1][h2:], T.sem.bdr, T.BT[:, 0:1], [T.bd[:, 0:1]])] if dn else []))
+    strips(lambda q, s, a: T[s][:, a:a + 16], nb)
+    n2 = V("ts", [p], T.n2[:], T.P[:], -2.0, None, A.add)
+    h = V("scan", [n2, kz], T.hp[:, 16:271], T.P[:, 0:255], T.n2[:, 1:256], -100.0, A.max, A.add)
+    v = V("scan", [], T.vp[:, 0:240], T.P[:, 0:240], T.n2[:, 16:256], -100.0, A.max, A.add)
+    h = V("memset", [h], T.hp[:, 31:272:16], 0.0)
+    v = V("ts", [v], T.vn[:, 16:256], T.vp[:, 0:240], -1.0, -3.0, A.is_equal, A.add)
+    h = V("ts", [h], T.m1[:], T.hp[:, 16:272], -1.0, None, A.is_equal)
+    v = V("scan", [v], T.v2[:], T.vn[:, 16:272], T.vn[:, 0:256], -100.0, A.max, A.add)
+    h = V("scan", [h], T.gh[:], T.half[:], T.m1[:], 0.0, A.mult, A.max)
+    V("memset", [], T.xp[:, 0:128] if dn else T.xp[:, 1088:1216], 0.0)
+    h = V("scan", [h, v], T.o2[:], T.gh[:], T.v2[:], -100.0, A.max, A.add)
+    load_w(0, [h])
+    l = V("ts", [h], T.l[:], T.o2[:], -5.6, U, A.is_gt, A.mult)
+    for t in range(4): mp = V("memset", [], T.xp[:, (192 if dn else 0) + t:1216 if dn else 1088:68], 0.0)
+
+    bdr = ("bdr", h2 * len([q for q in (r - 1, r + 1) if 0 <= q < N]))
+    a, b = (0 if up else 32), (64 if dn else 32)
+    if up: x = V("ts", [bdr], T.EL[:, 0:32], T.BT[:, 32:64], T.bd[:, 0:1], U, A.not_equal, A.mult)
+    if dn: x = V("ts", [bdr], T.EL[:, 32:64], T.BT[:, 0:32], T.bd[:, 8:9], U, A.not_equal, A.mult)
+    x = V("turn", [x], T.eb[:, a:b], T.EL[:, a:b])
+    if up: l = V("tt", [x, l], T.l[:, 0:16], T.l[:, 0:16], T.eb[:, 0:16], A.max)
+    if dn: l = V("tt", [x, l], T.l[:, 240:256], T.l[:, 240:256], T.eb[:, 32:48], A.max)
+    sS = V("scan", [l], T.S[:, 0:256], T.l[:], T.zb[:, 0:256], 0.0, A.add, A.add)
+    if ex_in: ft = V("turn", [], T.FT[:], T.l[:, 0:32])
+    wait("p", [sS])
+    down = others[::-1]
+    send([(down, e0, T.sem["inf%d" % r], T.S[:, 255:256], [T.inf[:, 8 * r:8 * r + 1]] * 3)])
+    if ex_in:
+        wait("p", [ft])
+        send([([r - 1], e0[h2:], T.sem.flg, T.FT[:, 0:1], [T.fl[:, 0:1]]),
+              (down, e0[:h2], T.sem.r0s, T.S[:, 15:16], [T.r0[:, 8 * r:8 * r + 1]] * 3)])
+    inf = [("inf%d" % q, ne) for q in range(N)]
+    r0s = ("r0s", h2 * (1 if ex_in else 2))
+    flg = ("flg", h2) if ex_out else None
+
+    sp = V("copy", [sS], T.S[:, 256:272], T.S[:, 15:256:16])
+    own = V("copy", [], T.inf[:, 8 * r:8 * r + 1], T.S[:, 255:256])
+    if ex_in: own = V("copy", [], T.r0[:, 8 * r:8 * r + 1], T.S[:, 15:16])
+    if ex_out: E1 = V("ts", [kS], T.E1[:], T.S[:, 255:256], 4.0, T.te[:], A.mult, A.add)
+    if dn: V("quant", [mz], T.padq[:, 416:544], T.pads[:, 416:544], T.zt[:, 0:512])
+    if ex_out: V("ts", [E1], T.E5[:], T.E1[:], 0.5, None, A.add)
+    a = 96 if dn else 128
+    pp = V("quant", [kX, mp], T.padq[:, a:a + 304], T.pads[:, a:a + 304], T.xp[:])
+    for k in (1, 2, 3): load_w(k, [pp])
+    quant_w(4)
+
+    if r == 0: tb, m = T.tp, kS
+    else:
+        tb = T.tb
+        i0, i1, i2 = T.inf[:, 0:1], T.inf[:, 8:9], T.inf[:, 16:17]
+        if r == 1:
+            V("ts", [kS, inf[0]], T.D[:], T.tp[:], i0, None, A.add)
+            x = V("ts", [], T.K[:], T.tp5[:], i0, None, A.add)
+            V("ts", [], T.De[:], i0, 4.0, T.E1[:], A.mult, A.add)
+        else:
+            a, b = (T.D, T.K) if r == 2 else (T.D0, T.D5)
+            V("ts", [kS, inf[0], inf[1]], a[:], T.tp[:], i0, i1, A.add, A.add)
+            x = V("ts", [], b[:], T.tp5[:], i0, i1, A.add, A.add)
+            if r == 3:
+                V("ts", [x, inf[2]], T.D[:], T.D0[:], i2, None, A.add)
+                x = V("ts", [], T.K[:], T.D5[:], i2, None, A.add)
+        m = V("tt", [x], T.tb[:], T.D[:], T.K[:], A.subtract)
+        if r == 1: k = V("ts", [], T.Ke[:], i0, 4.0, T.E5[:], A.mult, A.add)
+    if r == 0:
+        k = V("ts", [], T.Ke[:], T.E1[:], 0.5, None, A.add)
+        x = V("ts", [flg, kz], T.RB[:], T.zb[:, 0:32], T.fl[:, 0:1], None, A.add)
+        k = V("tt", [k], T.tbe[:], T.E1[:], T.Ke[:], A.subtract)
+        x = V("turn", [x], T.R16[:], T.RB[:])
+        sp = V("scan", [x], T.S[:, 272:288], T.R16[:, 0:16], T.zb[:, 0:16], T.S[:, 255:256], A.add, A.add)
+    al = S("sum", [sp, m], T.junk[:, 0:L], T.S[:, 0:L], 1.0, tb[:, 0:1], T.acl[:, 0:1])
+    y = V("ts", [sp, m], T.junk2[:, 0:L], T.S[:, 0:L], tb[:, 1:2], 0.0, A.add, A.is_lt)
+    if r == 1:
+        x = V("ts", [flg, kz], T.RB[:], T.zb[:, 0:32], T.fl[:, 0:1], None, A.add)
+        x = V("turn", [x], T.R16[:], T.RB[:])
+        k = V("tt", [k], T.tbe[:], T.De[:], T.Ke[:], A.subtract)
+    if ex_out:
+        k = V("scan", [x, k], T.Sl[:], T.R16[:, 0:16], T.zb[:, 0:16], 0.0, A.add, A.add)
+        ae = S("sum", [k], T.junk4[:], T.Sl[:], 4.0, T.tbe[:], T.ace[:])
+    y = V("scan", [y], T.junk3[:, 0:L], T.junk2[:, 0:L], T.zb[:, 0:L], -128.0, A.add, A.add)
+    x = V("ts", [y, kg], T.iof[:, 1:10:2], T.kv[:, 0:5], T.junk3[:, L - 1:L], None, A.add)
+    io = V("ts", [al], T.iof[:, 0:10:2], T.kk[:, 0:5], T.acl[:, 0:1], -0.5, A.add, A.mult)
+
+    def nio(q): return 11 if r == 1 or (r == 0 and q < 2) else 10
+    def ncs(s, q): return ne if q == (1 if s == 0 else (s + 3) % N) else h2
+    def block(t, k, q): return t[32 * k:32 * k + 32, 0:nio(q)]
+    def spread(q, out): return [S("act", [io], block(out, k, q), block(T.iof, q, q), F.Copy) for k in range(4)][-1]
+    def more(): return V("ts", [ae], T.iof[:, 10:11], T.ace[:], -0.5, PB + 255.0 + 8, A.mult, A.add)
+    if r == 1: io = more()
+    pls, pss = [], []
+    to = [2, 3, 1] if r == 0 else [(r + dq) % N for dq in range(1, N)]
+    OF = [T["of%d" % at(q, r)][:, 0:nio(q)] for q in to]
+    SP = [T["sp%d" % at(q, r)] for q in to]
+    z = [V("copy", [io], block(T["of%d" % at(to[0], r)], k, to[0]), block(T.iof, to[0], to[0])) for k in range(4)][-1:]
+    if r == 0: io2 = more()
+    for n in (1, 2):
+        if r == 0 and n == 2: io = io2
+        z.append(spread(to[n], SP[n]))
+    for n, q in enumerate(to):
+        i, j, nq = at(q, r), at(r, q), nio(q)
+        wd = 168 if nq == 11 else 160
+        pq = V("copy", [z[n], pp, hal], U32(T["pkq%d" % i][:, 0:16 * nq]), U32(T.padq[:]).indirect(OF[n]))
+        if n == 0:
+            for o in (1, 2): z[o] = V("copy", [z[o]], OF[o], SP[o][:, 0:nio(to[o])])
+        pss.append(S("act", [z[n], pp, hal], T["pks%d" % i][:, 0:16 * nq], T.pads[:].indirect(OF[n]), F.Copy))
+        pls.append(([q], eng[q][n * h2:n * h2 + h2] if n < 2 else eng[q], T.sem["cs%d" % j], T["pks%d" % i][:, 0:wd], [T.es[:, RG * r:RG * r + wd]]))
+        if n == 2:
+            wait("p", pss[1:2])
+            send(pls[:2])
+        wait("p", [pq])
+        send([([q], eng[q], T.sem["cq%d" % j], U8(T["pkq%d" % i][:, 0:wd]), [U8(T.eq[:, RG * r:RG * r + wd])])])
+    wait("p", pss[2:])
+    send(pls[2:])
+
+    z = spread(r, T.spo)
+    en = V("scan", [own] + inf[:r] + inf[r + 1:], T.en[:, 0:4], T.inf[:, 0:32:8], T.zb[:, 0:4], -0.5 * U, A.add, A.add)
+    x = V("tt", [en, r0s], T.en[:, 4:6], T.en[:, 0:2], T.r0[:, 8:17:8], A.add)
+    G = lambda c: T.g[:, 8 * c:8 * c + 8]
+    for n, c in ((4, 2), (5, 3), (0, 0), (2, 1), (1, 4), (3, 5)):
+        sg = S("sign", [x if c > 3 else en], G(n), T.nP[:], -1.0, T.en[:, c:c + 1])
+    ze = V("quant", [mz], T.eq[:, 4 * RG:4 * RG + 160], T.es[:, 4 * RG:4 * RG + 160], T.zt[:])
+    quant_w(0)
+    no = nio(r)
+    y = V("copy", [z], T.ioo[:, 0:no], T.spo[:, 0:no])
+    off = T.ioo[:, 0:no]
+    pe = V("copy", [y], U32(T.eq[:, RG * r:RG * r + 16 * no]), U32(T.padq[:]).indirect(off))
+    pf = S("act", [y], T.es[:, RG * r:RG * r + 16 * no], T.pads[:].indirect(off), F.Copy)
+    y = V("tt", [sg], T.gb[:], G(4), G(5), A.add)
+    b = V("tt", [], T.gac[:], T.g[:, 0:16], T.g[:, 16:32], A.add)
+    x = V("tt", [y], T.gs[:], T.slot[:], T.gb[:], A.subtract)
+    b = V("tt", [b], T.bb[:], T.gac[:, 0:8], T.gac[:, 8:16], A.subtract) if r < 2 else V("tt", [b], T.bb[:], G(2), G(3), A.subtract)
+    V("tt", [x], T.b1[:], T.gs[:], T.gac[:, 8:16], A.subtract)
+    b = V("tt", [b], T.uu[:], T.bb[:], T.cE[:], A.mult)
+    V("tt", [], T.bf[:, 0:8], T.gs[:], T.gac[:, 0:8], A.subtract)
+    b = V("tt", [b], T.bf[:, 8:16], T.b1[:], T.uu[:], A.subtract)
+    fd = V("ts", [b], T.fo[:], T.bf[:], RG / 2.0, None, A.mult)
+    quant_w(1)
+
+    cq = [("cq%d" % at(q, r), ne) for q in others]
+    cs = [("cs%d" % at(q, r), ncs(q, r)) for q in others]
+    for n, k in enumerate((1, 3, 4, 0, 2)):
+        lo, hi = 128 * n, 128 * n + 128
+        s = slice(32 * k, 32 * k + 4 * RG + 32)
+        off = T.fo[:, 8:16] if k == 3 else T.fo[:, 0:8]
+        if n in (2, 3): quant_w(n)
+        a = V("copy", [pe, fd] + cq, U32(T.xfq[:, lo:hi]), U32(T.eq[:, s]).indirect(off))
+        b = S("act", [pf, fd, ze] + cs, T.xfs[:, lo:hi], T.es[:, s].indirect(off), F.Copy)
+        ms = []
+        for o in range(2):
+            w = 128 * (2 * n + o)
+            ms.append(op("t", "mm", [a, b, qw[n]], T.yp[:, 512 * o:512 * o + 128],
+                         T.wq[:, w:w + 128], T.ws[:, w:w + 128], T.xfq[:, lo:hi], T.xfs[:, lo:hi], n == 0, n == 4))
+    x = V("copy", [ms[0]], T.ys[:, 0:128], T.yp[:, 0:128])
+    dma("s", "st0", [x], T.y[:, 0:128], T.ys[:, 0:128])
+    x = S("act", [ms[1]], T.ys[:, 128:256], T.yp[:, 512:640], F.Copy)
+    dma("a", "st1", [x], T.y[:, 128:256], T.ys[:, 128:256])
+    wait("p", [(k, n) for k, n in cnt.items()])
+    wait("p", [hal, bdr, flg, r0s] + inf[:r] + inf[r + 1:])

@@ -5,7 +5,9 @@ A = AluOpType
 F = ActivationFunctionType
 CODE = "float8_e4m3fn_x4"
 RG = 176
-U = 1.0 / 128
+M128 = 24576.0
+M32 = 6144.0
+YW = 300
 
 
 def sb(n, d="float32"): return ("sbuf", [128, n], d)
@@ -13,25 +15,20 @@ def sb(n, d="float32"): return ("sbuf", [128, n], d)
 
 BF, I32, U16 = "bfloat16", "int32", "uint16"
 SCRATCH = {
-    "ut": sb(512, BF), "xt": sb(1024, BF), "wt": sb(5120, BF), "zt": sb(640, BF), "xp": sb(1216, BF),
-    "uq": sb(128, CODE), "us": sb(128, "uint8"), "urq": sb(128, CODE), "urs": sb(128, "uint8"),
+    "ut": sb(8, BF), "ur": sb(512, BF), "xt": sb(1024, BF), "wt": sb(5120, BF), "zt": sb(640, BF), "xp": sb(1216, BF),
+    "urq": sb(128, CODE), "urs": sb(128, "uint8"),
     "xq": sb(256, CODE), "xs": sb(256, "uint8"), "padq": sb(544, CODE), "pads": sb(544, "uint8"),
     "wq": sb(1280, CODE), "ws": sb(1280, "uint8"),
     "eq": sb(4 * RG + 160, CODE), "es": sb(4 * RG + 160, "uint8"),
-    "xfq": sb(640, CODE), "xfs": sb(640, "uint8"),
-    "off0": sb(8, U16), "ys": sb(256),
+    "xfq": sb(640, CODE), "xfs": sb(640, "uint8"), "ys": sb(256),
     "sc": ("psum", [128, 1024], "float32"), "yp": ("psum", [128, 1024], "float32"),
-    "pI": sb(1, I32), "pm": sb(4, I32), "pf": sb(4), "i64": sb(8), "i16": sb(8), "kk": sb(8), "kv": sb(8),
-    "b2": sb(1), "b3": sb(1), "nb3": sb(1), "nb2": sb(1), "b7": sb(1), "p16": sb(1), "x8": sb(1),
-    "tp": sb(2), "tp5": sb(2), "te": sb(1), "nP": sb(8), "slot": sb(8), "cE": sb(8), "half": sb(256, BF), "zb": sb(288, BF),
-    "B": sb(64, BF), "BT": sb(64, BF), "EL": sb(64, BF), "eb": sb(64, BF),
-    "P": sb(256, BF), "n2": sb(256, BF), "hp": sb(288, BF), "vp": sb(256, BF), "vn": sb(272, BF), "m1": sb(256, BF), "gh": sb(256, BF),
-    "v2": sb(256, BF), "o2": sb(256, BF), "l": sb(256, BF), "S": sb(288, BF), "FT": sb(32, BF), "RB": sb(32, BF), "R16": sb(32, BF), "Sl": sb(16, BF),
-    "bd": sb(16, BF), "inf": sb(32, BF), "r0": sb(32, BF), "fl": sb(8, BF),
-    "D": sb(2), "D0": sb(2), "D5": sb(2), "K": sb(2, I32), "tb": sb(2), "E1": sb(1), "E5": sb(1), "De": sb(1), "Ke": sb(1, I32), "tbe": sb(1),
-    "junk": sb(288, BF), "junk2": sb(288, BF), "junk3": sb(288, BF), "junk4": sb(16, BF), "acl": sb(2), "ace": sb(1), "iof": sb(12),
-    "en": sb(6), "g": sb(48), "gac": sb(16), "gb": sb(8), "gs": sb(8), "b1": sb(8), "bb": sb(8), "uu": sb(8), "bf": sb(16),
-    "fo": sb(16, U16), "ioo": sb(12, U16), "spo": sb(12),
+    "pI": sb(1, I32), "pm": sb(4, I32), "pf": sb(4), "i16": sb(16), "i64": sb(2), "nI": sb(128), "nP": sb(128), "W": sb(128),
+    "b2": sb(1), "b3": sb(1), "na": sb(1), "ka": sb(1), "kb": sb(1), "tp": sb(2), "o7": sb(8, U16), "zb": sb(16, BF),
+    "s": sb(276, BF), "s2": sb(256, BF), "B": sb(64, BF), "BT": sb(64, BF), "H": sb(274, BF), "A2": sb(256, BF), "T2": sb(256, BF),
+    "TT": sb(64, BF), "fa": sb(256, BF), "fb": sb(256, BF), "Si": sb(256, BF), "S": sb(288, BF), "EL": sb(64, BF), "eb": sb(64, BF),
+    "bd": sb(16, BF), "fl": sb(8, BF), "inf": sb(256), "ini": sb(2), "th2": sb(1, BF), "E1": sb(1), "ik": sb(2), "ike": sb(1), "RB": sb(32, BF), "R16": sb(32, BF), "Sl": sb(16, BF),
+    "D": sb(2), "K": sb(2, BF), "De": sb(1), "Ke": sb(1, BF), "Y": sb(2 * YW, BF), "Ye": sb(16, BF), "J": sb(YW, BF),
+    "thr": sb(8), "G": sb(128), "Fo": sb(128), "fo": sb(16, U16), "ioo": sb(12, U16), "spo": sb(12),
 }
 for _i in range(3):
     SCRATCH["of%d" % _i] = sb(12, U16)
@@ -39,7 +36,7 @@ for _i in range(3):
     SCRATCH["pkq%d" % _i] = sb(RG, CODE)
     SCRATCH["pks%d" % _i] = sb(RG, "uint8")
 SEMAPHORES = ["vc", "ac", "tc", "pc", "ldu", "ldxa", "ldxb", "ldw0", "ldw1", "ldw2", "ldw3", "ldw4", "halo", "bdr", "inf0", "inf1", "inf2", "inf3",
-              "r0s", "flg", "cq0", "cq1", "cq2", "cs0", "cs1", "cs2", "sent", "st0", "st1"]
+              "flg", "cq0", "cq1", "cq2", "cs0", "cs1", "cs2", "sent", "st0", "st1"]
 
 
 def rank_program(g, core, T, topo):
@@ -74,8 +71,6 @@ def rank_program(g, core, T, topo):
         elif name == "quant": i = q.quantize_mx(*args)
         elif name == "act": i = q.activation(*args)
         elif name == "lin": i = q.activation(args[0], args[1], F.Identity, bias=args[3], scale=args[2])
-        elif name == "sign": i = q.activation(args[0], args[1], F.Sign, bias=args[3], scale=args[2])
-        elif name == "sum": i = q.activation(args[0], args[1], F.Sign, bias=args[3], scale=args[2], accum_out=args[4])
         elif name == "mm": i = q.matmul_mx(*args)
         elif name == "iota": i = q.iota(*args)
         else: i = q.iota(*args, allow_small_or_imprecise_dtypes=True)
@@ -111,179 +106,189 @@ def rank_program(g, core, T, topo):
     ex_out, ex_in = r in (0, 1), r in (1, 2)
     PB = 128 if dn else 129
     L = 288 if r == 0 else 272
-    ldu = dma("a", "ldu", [], T.ut[:, 0:8], T.u[:, 0:8])
-    h0, h1 = (0, 1) if up else (1, 0)
-    X = lambda h: slice(512 * h, 512 * h + 512)
-    ldxa = dma("s", "ldxa", [], T.xt[:, X(h0)], T.x[:, X(h0)])
-    ldxb = dma("a", "ldxb", [], T.xt[:, X(h1)], T.x[:, X(h1)])
+    ldu = dma("a", "ldu", [], T.ut[:], T.u[:, 0:8])
+    dma("s", "ldxa", [], T.xt[:, 256:512], T.x[:, 0:256])
+    ldxa = dma("a", "ldxa", [], T.xt[:, 0:256], T.x[:, 768:1024])
+    ldxb = dma("s", "ldxb", [], T.xt[:, 512:1024], T.x[:, 256:768])
     kp = op("p", "iota", [], T.pI[:], [[0, 1]], 0, 1)
-    op("p", "iotaf", [], T.i64[:], [[64, 8]], 0, 0)
-    op("p", "iotaf", [], T.i16[:], [[0, 4], [16, 2]], 0, 0)
-    op("p", "iotaf", [], T.kk[:, 0:3], [[-2, 3]], -2 * (PB - 1) - L, 0)
-    op("p", "iotaf", [], T.kk[:, 3:5], [[-68, 2]], -2 * (PB - 17) - L, 0)
-    op("p", "iotaf", [], T.kv[:, 0:3], [[1, 3]], PB - 1 + 128, 0)
-    kg = op("p", "iotaf", [], T.kv[:, 3:5], [[34, 2]], PB - 17 + 128, 0)
-    mu = V("memset", [], T.ut[:, 8:512], 0.0)
-    mo = V("memset", [], T.off0[:], 0)
+    op("p", "iotaf", [], T.i16[:], [[0, 8], [16, 2]], 0, 0)
+    if r == 0: op("p", "iotaf", [], T.i64[:], [[64, 2]], -64, 0)
+    op("p", "iotaf", [], T.W[:], [[0, 64], [-RG, 2]], RG, 0)
+    kg = op("p", "iotaf", [], T.nI[:], [[0, 2], [64, 8], [0, 8]], 8 * r, 0)
+    mz = V("memset", [], T.zt[:], 0.0)
     V("ts", [kp], T.pm[:, 3:4], T.pI[:], 5, None, A.logical_shift_right)
     V("ts", [], T.pm[:, 0:1], T.pI[:], 15, None, A.bitwise_and)
     V("ts", [], T.pm[:, 1:2], T.pI[:], 7, None, A.bitwise_and)
     k = V("ts", [], T.pm[:, 2:3], T.pI[:], 3, 1, A.logical_shift_right, A.bitwise_and)
-    mB = V("memset", [], T.B[:], 0.0)
+    V("memset", [], T.s[:, 0:3], 0.0)
+    V("memset", [], T.s[:, 275:276], 0.0)
+    V("memset", [], T.zb[:], 0.0)
     kf = V("copy", [k], T.pf[:], T.pm[:])
-    mz = V("memset", [], T.zt[:], 0.0)
+    ze = V("quant", [], T.eq[:, 4 * RG:4 * RG + 160], T.es[:, 4 * RG:4 * RG + 160], T.zt[:])
 
-    qu = V("quant", [ldu, mu], T.uq[:], T.us[:], T.ut[:])
-    pu = V("copy", [qu, mo], U32(T.urq[:]), U32(T.uq[:]).indirect(T.off0[:]))
-    pv = S("act", [qu, mo], T.urs[:], T.us[:].indirect(T.off0[:]), F.Copy)
+    for t in range(4): k = V("ts", [ldu], T.ur[:, t:512:4], T.zt[:, 0:128], T.ut[:, t:t + 1], None, A.add)
+    if dn: V("quant", [], T.padq[:, 416:544], T.pads[:, 416:544], T.zt[:, 0:512])
+    qu = V("quant", [k], T.urq[:], T.urs[:], T.ur[:])
     qx, mm = {}, {}
 
     def score(h, ld):
         c = slice(128 * h, 128 * h + 128)
-        qx[h] = V("quant", [ld], T.xq[:, c], T.xs[:, c], T.xt[:, X(h)])
-        mm[h] = op("t", "mm", [pu, pv, qx[h]], T.sc[:, 512 * h:512 * h + 128], T.urq[:], T.urs[:], T.xq[:, c], T.xs[:, c], True, True)
-    score(h0, ldxa)
-    V("memset", [], T.half[:], 0.5)
-    V("memset", [], T.vn[:, 0:16], -3.0)
-    V("memset", [], T.vn[:, 256:272], -3.0)
-    kz = V("memset", [], T.zb[:], 0.0)
-    score(h1, ldxb)
+        qx[h] = V("quant", [ld], T.xq[:, c], T.xs[:, c], T.xt[:, 512 * h:512 * h + 512])
+        mm[h] = op("t", "mm", [qu, qx[h]], T.sc[:, 512 * h:512 * h + 128], T.urq[:], T.urs[:], T.xq[:, c], T.xs[:, c], True, True)
+    score(0, ldxa)
+    k = V("memset", [], T.Y[:, L:L + 10], 0.0)
+    k = V("memset", [], T.Y[:, YW + L:YW + L + 10], 0.0)
+    V("memset", [], T.thr[:, 5:6], 0.0)
+    V("memset", [], T.thr[:, 7:8], 1e9)
+    score(1, ldxb)
     ldw, qw = {}, {}
 
     def load_w(k, deps): ldw[k] = dma("s", "ldw%d" % k, deps, T.wt[:, 1024 * k:1024 * k + 1024], T.w[:, 1024 * k:1024 * k + 1024])
-    def quant_w(k): qw[k] = V("quant", [ldw[k]], T.wq[:, 256 * k:256 * k + 256], T.ws[:, 256 * k:256 * k + 256], T.wt[:, 1024 * k:1024 * k + 1024])
-    load_w(4, [ldxb])
+    def quant_w(n): qw[n] = V("quant", [ldw[n // 2]], T.wq[:, 128 * n:128 * n + 128], T.ws[:, 128 * n:128 * n + 128], T.wt[:, 512 * n:512 * n + 512])
+    load_w(0, [ldxb])
 
-    nb = ([(r - 1, 0, 400)] if up else []) + ([(r + 1, 240, 112)] if r == N - 2 else [])
+    nb = ([(r - 1, 64, 400)] if up else []) + ([(r + 1, 48, 112)] if r == N - 2 else [])
 
-    def strips(view, nb):
+    def strips(view):
         if nb:
-            send([([q], eng[q][(src > 0) * h2:(src > 0) * h2 + h2], T.sem.halo, view("xq", "xs", src), [view("padq", "pads", dst)]) for q, src, dst in nb])
-    for b in nb:
-        wait("p", [qx[b[1] > 0]])
-        strips(lambda q, s, a: U8(T[q][:, a:a + 16]), [b])
+            send([([q], eng[q][n * h2:n * h2 + h2], T.sem.halo, view("xq", "xs", src), [view("padq", "pads", dst)]) for n, (q, src, dst) in enumerate(nb)])
+    wait("p", [qx[0]])
+    strips(lambda q, s, a: U8(T[q][:, a:a + 16]))
     hal = ("halo", 2 * h2)
 
-    S("lin", [kf, kg], T.b2[:], T.pf[:, 2:3], 32.0, T.pf[:, 1:2])
-    k = S("lin", [], T.p16[:], T.pf[:, 0:1], 2.0 / RG, 4 + 0.5 / RG)
-    k = S("lin", [k], T.b3[:], T.pf[:, 3:4], 8.0, T.b2[:])
-    k = S("lin", [k], T.nb3[:], T.b3[:], -U, -0.5 * U)
-    S("lin", [], T.x8[:], T.pf[:, 2:3], -8.0 / RG, 64.0 / RG)
-    k = S("lin", [k], T.tp[:], T.i64[:, 0:2], -U, T.nb3[:])
-    S("lin", [], T.b7[:], T.pf[:, 3:4], 8.0, T.pf[:, 1:2])
-    k = S("lin", [k], T.tp5[:], T.tp[:], 1.0, 0.5)
-    S("lin", [], T.nb2[:], T.b2[:], U, 8.0 * r * U)
-    S("lin", [k], T.te[:], T.b7[:], -1.0 / 32, -0.5 / 32)
-    k = S("lin", [], T.slot[:], T.i16[:], 2.0 / RG, T.p16[:])
-    S("lin", [k], T.nP[:], T.i64[:], U, T.nb2[:])
-    kS = S("lin", [], T.cE[:], T.i16[:], -1.0 / RG, T.x8[:])
+    if r == 0:
+        k = S("lin", [kf, kg], T.b2[:], T.pf[:, 2:3], 32.0, T.pf[:, 1:2])
+        k = S("lin", [k], T.b3[:], T.pf[:, 3:4], 8.0, T.b2[:])
+        k = S("lin", [k], T.b2[:], T.b3[:], -1.0, M128 + 63.5)
+        k = S("lin", [k], T.tp[:], T.i64[:], 1.0, T.b2[:])
+        kt = S("lin", [k], T.K[:], T.tp[:], 1.0, 0.0)
+    S("lin", [kf, kg], T.na[:], T.pf[:, 3:4], -8.0, M128 + 63.5)
+    S("lin", [], T.ka[:], T.pf[:, 2:3], 8.0, RG - 64.0)
+    k = S("lin", [], T.kb[:], T.pf[:, 2:3], -8.0, 64.0)
+    S("lin", [], T.W[:, 7:128:8], T.i16[:], 1.0, T.pf[:, 0:1])
+    S("lin", [k], T.nP[:], T.nI[:], 1.0, T.na[:])
+    for j in (3, 5):
+        plain = j == 5 and r >= 2
+        S("lin", [], T.W[:, 64 + j:128:8], T.i16[:, 0:8], 0.0 if plain else 1.0, float(RG) if plain else T.ka[:])
+        kS = S("lin", [], T.W[:, 65 + j:128:8], T.i16[:, 0:8], 0.0 if plain else -1.0, 0.0 if plain else T.kb[:])
     xp0 = 128 if dn else 4
-    for i in range(16): kX = S("act", [ldxa, ldxb], T.xp[:, xp0 + 68 * i:xp0 + 68 * i + 64], T.xt[:, 64 * i:64 * i + 64], F.Copy)
+    for i in range(16):
+        a = 64 * ((i + 4) % 16)
+        kX = S("act", [ldxa, ldxb], T.xp[:, xp0 + 68 * i:xp0 + 68 * i + 64], T.xt[:, a:a + 64], F.Copy)
 
-    if up: kb = V("ts", [mm[0], mB], T.B[:, 32:48], T.sc[:, 0:16], 0.0, None, A.is_gt)
-    if dn: kb = V("ts", [mm[1], mB], T.B[:, 0:16], T.sc[:, 624:640], 0.0, None, A.is_gt)
+    V("ts", [mm[0]], T.B[:, 0:32], T.sc[:, 48:80], 1.0 / 32, -1.0 / 32, A.min, A.max)
+    kb = V("ts", [], T.B[:, 32:64], T.sc[:, 48:80], 6.25 / 32, -9.75 / 32, A.min, A.max)
+
+    def signs(out, a, b, k, deps): return V("ts", deps, out, T.sc[:, a:b], 0.0, k, A.is_gt, A.add)
+    signs(T.s[:, 3:19], 64, 80, -0.5, [])
+    signs(T.s[:, 19:83], 64, 128, -0.5, [])
+    signs(T.s[:, 211:275], 0, 64, -0.5, [])
     kb = V("turn", [kb], T.BT[:], T.B[:])
-    for h in (h0, h1): p = V("ts", [mm[h]], T.P[:, 128 * h:128 * h + 128], T.sc[:, 512 * h:512 * h + 128], 0.0, None, A.is_gt)
+    signs(T.s2[:, 0:48], 80, 128, 7.5, [])
+    signs(T.s2[:, 176:240], 0, 64, 7.5, [])
+    signs(T.s2[:, 240:256], 48, 64, 7.5, [])
+    signs(T.s[:, 83:211], 512, 640, -0.5, [mm[1]])
+    p = signs(T.s2[:, 48:176], 512, 640, 7.5, [])
     wait("p", [kb])
-    send(([([r - 1], eng[r - 1][:h2], T.sem.bdr, T.BT[:, 32:33], [T.bd[:, 8:9]])] if up else [])
-         + ([([r + 1], eng[r + 1][h2:], T.sem.bdr, T.BT[:, 0:1], [T.bd[:, 0:1]])] if dn else []))
-    strips(lambda q, s, a: T[s][:, a:a + 16], nb)
-    n2 = V("ts", [p], T.n2[:], T.P[:], -2.0, None, A.add)
-    h = V("scan", [n2, kz], T.hp[:, 16:271], T.P[:, 0:255], T.n2[:, 1:256], -100.0, A.max, A.add)
-    v = V("scan", [], T.vp[:, 0:240], T.P[:, 0:240], T.n2[:, 16:256], -100.0, A.max, A.add)
-    h = V("memset", [h], T.hp[:, 31:272:16], 0.0)
-    v = V("ts", [v], T.vn[:, 16:256], T.vp[:, 0:240], -1.0, -3.0, A.is_equal, A.add)
-    h = V("ts", [h], T.m1[:], T.hp[:, 16:272], -1.0, None, A.is_equal)
-    v = V("scan", [v], T.v2[:], T.vn[:, 16:272], T.vn[:, 0:256], -100.0, A.max, A.add)
-    h = V("scan", [h], T.gh[:], T.half[:], T.m1[:], 0.0, A.mult, A.max)
-    V("memset", [], T.xp[:, 0:128] if dn else T.xp[:, 1088:1216], 0.0)
-    h = V("scan", [h, v], T.o2[:], T.gh[:], T.v2[:], -100.0, A.max, A.add)
-    load_w(0, [h])
-    l = V("ts", [h], T.l[:], T.o2[:], -5.6, U, A.is_gt, A.mult)
-    for t in range(4): mp = V("memset", [], T.xp[:, (192 if dn else 0) + t:1216 if dn else 1088:68], 0.0)
+    send(([([r - 1], eng[r - 1][:h2], T.sem.bdr, T.BT[:, 31:33], [T.bd[:, 8:10]])] if up else [])
+         + ([([r + 1], eng[r + 1][h2:], T.sem.bdr, T.BT[:, 31:33], [T.bd[:, 0:2]])] if dn else []))
+    strips(lambda q, s, a: T[s][:, a:a + 16])
+    for j, d in ((1, -1.0), (3, 1.0), (7, -18.0)): V("memset", [], T.Y[:, L + j:2 * YW:YW], -128 * d)
+
+    k = V("scan", [p], T.H[:, 0:273], T.s[:, 3:276], T.s[:, 0:273], 0.0, A.add, A.subtract)
+    V("scan", [], T.A2[:], T.s[:, 3:259], T.s2[:], 100.0, A.min, A.add)
+    V("tt", [k], T.H[:, 17:273:16], T.s[:, 19:275:16], T.s[:, 20:276:16], A.add)
+    k = V("tt", [], T.H[:, 32:273:16], T.s[:, 33:275:16], T.s[:, 34:275:16], A.add)
+    for j, d in ((5, 1.0), (9, 34.0)): V("memset", [], T.Y[:, L + j:2 * YW:YW], -128 * d)
+    ko = V("ts", [], T.o7[:], T.zb[:, 0:8], T.pf[:, 1:2], 7.0, A.subtract, A.add)
+    k = V("scan", [k], T.T2[:], T.H[:, 17:273], T.A2[:], 100.0, A.min, A.add)
+    load_w(1, [k])
+    for t in range(3): V("memset", [], T.xp[:, (192 if dn else 0) + t:1216 if dn else 1088:68], 0.0)
+    if up: tt = V("turn", [k], T.TT[:, 32:64], T.T2[:, 0:32])
+    if ex_in:
+        wait("p", [tt])
+        send([([r - 1], e0[:h2], T.sem.flg, T.TT[:, 32:33], [T.fl[:, 0:1]])])
+    if dn: tt = V("turn", [k], T.TT[:, 0:32], T.T2[:, 224:256])
+    V("ts", [], T.fa[:], T.T2[:], 6.25, None, A.is_gt)
+    k = V("ts", [], T.fb[:], T.T2[:], 9.75, None, A.is_gt)
 
     bdr = ("bdr", h2 * len([q for q in (r - 1, r + 1) if 0 <= q < N]))
-    a, b = (0 if up else 32), (64 if dn else 32)
-    if up: x = V("ts", [bdr], T.EL[:, 0:32], T.BT[:, 32:64], T.bd[:, 0:1], U, A.not_equal, A.mult)
-    if dn: x = V("ts", [bdr], T.EL[:, 32:64], T.BT[:, 0:32], T.bd[:, 8:9], U, A.not_equal, A.mult)
+    a, b = (0 if dn else 32), (64 if up else 32)
+    if dn: x = V("ts", [bdr, tt], T.EL[:, 0:32], T.TT[:, 0:32], T.bd[:, 8:9], T.bd[:, 9:10], A.mult, A.is_le)
+    if up: x = V("ts", [bdr, tt], T.EL[:, 32:64], T.TT[:, 32:64], T.bd[:, 0:1], T.bd[:, 1:2], A.mult, A.is_le)
+    si = V("scan", [k], T.Si[:], T.fa[:], T.fb[:], 0.0, A.add, A.subtract)
     x = V("turn", [x], T.eb[:, a:b], T.EL[:, a:b])
-    if up: l = V("tt", [x, l], T.l[:, 0:16], T.l[:, 0:16], T.eb[:, 0:16], A.max)
-    if dn: l = V("tt", [x, l], T.l[:, 240:256], T.l[:, 240:256], T.eb[:, 32:48], A.max)
-    sS = V("scan", [l], T.S[:, 0:256], T.l[:], T.zb[:, 0:256], 0.0, A.add, A.add)
-    if ex_in: ft = V("turn", [], T.FT[:], T.l[:, 0:32])
-    wait("p", [sS])
-    down = others[::-1]
-    send([(down, e0, T.sem["inf%d" % r], T.S[:, 255:256], [T.inf[:, 8 * r:8 * r + 1]] * 3)])
-    if ex_in:
-        wait("p", [ft])
-        send([([r - 1], e0[h2:], T.sem.flg, T.FT[:, 0:1], [T.fl[:, 0:1]]),
-              (down, e0[:h2], T.sem.r0s, T.S[:, 15:16], [T.r0[:, 8 * r:8 * r + 1]] * 3)])
+    x15, x0, c0 = T.eb[:, 16:32], T.eb[:, 32:48], 64 * r
+    V("memset", [], T.xp[:, (192 if dn else 0) + 3:1216 if dn else 1088:68], 0.0)
+    mp = V("memset", [], T.xp[:, 0:128] if dn else T.xp[:, 1088:1216], 0.0)
+    if r == 0:
+        k = V("ts", [si, kt], T.ini[:], T.tp[:], T.Si[:, 255:256], None, A.add)
+        for c in (0, 1): own = V("scan", [x, k], T.inf[:, 32 + c:64:2], x15, T.zb[:], T.ini[:, c:c + 1], A.add, A.add)
+    else:
+        if dn: V("scan", [x, si], T.inf[:, c0 + 32:c0 + 64:2], x0, T.zb[:], T.Si[:, 15:16], A.add, A.add)
+        own = V("scan", [x, si], T.inf[:, c0 + 33:c0 + 64:2], x0, x15 if dn else T.zb[:], T.Si[:, 255:256], A.add, A.add)
+    wait("p", [own])
+    msg = T.inf[:, c0 + (62 if dn else 63):c0 + 64]
+    send([(others[::-1], e0, T.sem["inf%d" % r], msg, [msg] * 3)])
     inf = [("inf%d" % q, ne) for q in range(N)]
-    r0s = ("r0s", h2 * (1 if ex_in else 2))
     flg = ("flg", h2) if ex_out else None
 
-    sp = V("copy", [sS], T.S[:, 256:272], T.S[:, 15:256:16])
-    own = V("copy", [], T.inf[:, 8 * r:8 * r + 1], T.S[:, 255:256])
-    if ex_in: own = V("copy", [], T.r0[:, 8 * r:8 * r + 1], T.S[:, 15:16])
-    if ex_out: E1 = V("ts", [kS], T.E1[:], T.S[:, 255:256], 4.0, T.te[:], A.mult, A.add)
-    if dn: V("quant", [mz], T.padq[:, 416:544], T.pads[:, 416:544], T.zt[:, 0:512])
-    if ex_out: V("ts", [E1], T.E5[:], T.E1[:], 0.5, None, A.add)
+    if up: k = V("tt", [], T.fa[:, 0:16], T.fa[:, 0:16], x0, A.add)
+    if dn: k = V("tt", [], T.fa[:, 240:256], T.fa[:, 240:256], x15, A.add)
+    load_w(2, [k])
+    if ex_out:
+        x = S("lin", [kb], T.th2[:], T.BT[:, 32:33], 1.0, 3.5 / 32)
+        x = V("ts", [flg, x], T.RB[:], T.BT[:, 0:32], T.fl[:, 0:1], T.th2[:], A.mult, A.is_lt)
+    quant_w(0)
+    k = V("scan", [k], T.S[:, 0:256], T.fa[:], T.fb[:], 0.0, A.add, A.subtract)
+    te = M128 + 62 - 4 * (M128 + 63.5)
+    if r == 0: E1 = V("memset", [], T.E1[:], te)
+    if r == 1: E1 = V("ts", [own], T.E1[:], T.inf[:, 127:128], 4.0, te, A.mult, A.add)
+    if ex_out: x = V("turn", [x], T.R16[:], T.RB[:])
+    quant_w(1)
+    sp = V("copy", [k], T.S[:, 256:272], T.S[:, 15:256:16])
+    if r == 0: sp = V("scan", [x], T.S[:, 272:288], T.R16[:, 0:16], T.zb[:], T.S[:, 255:256], A.add, A.add)
+    if ex_out: sp = V("scan", [x], T.Sl[:], T.R16[:, 0:16], T.zb[:], 0.0, A.add, A.add)
     a = 96 if dn else 128
     pp = V("quant", [kX, mp], T.padq[:, a:a + 304], T.pads[:, a:a + 304], T.xp[:])
-    for k in (1, 2, 3): load_w(k, [pp])
-    quant_w(4)
+    for k in (3, 4): load_w(k, [pp])
 
-    if r == 0: tb, m = T.tp, kS
-    else:
-        tb = T.tb
-        i0, i1, i2 = T.inf[:, 0:1], T.inf[:, 8:9], T.inf[:, 16:17]
-        if r == 1:
-            V("ts", [kS, inf[0]], T.D[:], T.tp[:], i0, None, A.add)
-            x = V("ts", [], T.K[:], T.tp5[:], i0, None, A.add)
-            V("ts", [], T.De[:], i0, 4.0, T.E1[:], A.mult, A.add)
-        else:
-            a, b = (T.D, T.K) if r == 2 else (T.D0, T.D5)
-            V("ts", [kS, inf[0], inf[1]], a[:], T.tp[:], i0, i1, A.add, A.add)
-            x = V("ts", [], b[:], T.tp5[:], i0, i1, A.add, A.add)
-            if r == 3:
-                V("ts", [x, inf[2]], T.D[:], T.D0[:], i2, None, A.add)
-                x = V("ts", [], T.K[:], T.D5[:], i2, None, A.add)
-        m = V("tt", [x], T.tb[:], T.D[:], T.K[:], A.subtract)
-        if r == 1: k = V("ts", [], T.Ke[:], i0, 4.0, T.E5[:], A.mult, A.add)
-    if r == 0:
-        k = V("ts", [], T.Ke[:], T.E1[:], 0.5, None, A.add)
-        x = V("ts", [flg, kz], T.RB[:], T.zb[:, 0:32], T.fl[:, 0:1], None, A.add)
-        k = V("tt", [k], T.tbe[:], T.E1[:], T.Ke[:], A.subtract)
-        x = V("turn", [x], T.R16[:], T.RB[:])
-        sp = V("scan", [x], T.S[:, 272:288], T.R16[:, 0:16], T.zb[:, 0:16], T.S[:, 255:256], A.add, A.add)
-    al = S("sum", [sp, m], T.junk[:, 0:L], T.S[:, 0:L], 1.0, tb[:, 0:1], T.acl[:, 0:1])
-    y = V("ts", [sp, m], T.junk2[:, 0:L], T.S[:, 0:L], tb[:, 1:2], 0.0, A.add, A.is_lt)
-    if r == 1:
-        x = V("ts", [flg, kz], T.RB[:], T.zb[:, 0:32], T.fl[:, 0:1], None, A.add)
-        x = V("turn", [x], T.R16[:], T.RB[:])
-        k = V("tt", [k], T.tbe[:], T.De[:], T.Ke[:], A.subtract)
+    i0, i1, i2 = T.inf[:, 62:64], T.inf[:, 127:128], T.inf[:, 191:192]
+    d0, m = (63 if r == 1 else 1), None
+    if r == 1: m = V("copy", inf[:1], T.K[:], i0)
+    for out in (T.K, T.D):
+        if r == 2: m = V("ts", inf[:2], out[:], i0, i1, None, A.add)
+        if r == 3: m = V("ts", inf[:3], out[:], i0, i1, i2, A.add, A.add)
+    for out in (T.Ke, T.De):
+        if ex_out: m = V("ts", [E1], out[:], T.inf[:, 63:64], 4.0, T.E1[:], A.mult, A.add)
+    if r > 1: quant_w(2)
+    def rounded(c): return V("ts", [sp, m if r > 1 else None], T.Y[:, YW * c:YW * c + L], T.S[:, 0:L], (T.tp, T.inf, T.D, T.D)[r][:, d0 - c:d0 - c + 1],
+                             M128 + (128 if r == 0 else 1024), A.add, A.min)
+    rounded(1)
+    V("ts", [m], T.ik[:], T.K[:], -float(L), -128.0 * (PB - 256 + L), A.mult, A.add)
     if ex_out:
-        k = V("scan", [x, k], T.Sl[:], T.R16[:, 0:16], T.zb[:, 0:16], 0.0, A.add, A.add)
-        ae = S("sum", [k], T.junk4[:], T.Sl[:], 4.0, T.tbe[:], T.ace[:])
-    y = V("scan", [y], T.junk3[:, 0:L], T.junk2[:, 0:L], T.zb[:, 0:L], -128.0, A.add, A.add)
-    x = V("ts", [y, kg], T.iof[:, 1:10:2], T.kv[:, 0:5], T.junk3[:, L - 1:L], None, A.add)
-    io = V("ts", [al], T.iof[:, 0:10:2], T.kk[:, 0:5], T.acl[:, 0:1], -0.5, A.add, A.mult)
+        V("ts", [], T.Ye[:], T.Sl[:], 4.0, T.De[:], A.mult, A.add)
+        x = V("ts", [], T.ike[:], T.Ke[:], -16.0, -128.0 * (PB + 15), A.mult, A.add)
+    y = rounded(0)
+    if ex_out: y = V("scan", [x], T.J[:, L - 4:L + 11:2], T.Ye[:, 0:16:2], T.Ye[:, 1:16:2], T.ike[:], A.add, A.add)
+    if r < 2: quant_w(2)
+    else: quant_w(3)
+    for c in (1, 0):
+        a = YW * c
+        io = V("scan", [y], T.J[:, c:L + 10:2], T.Y[:, a:a + L + 10:2], T.Y[:, a + 1:a + L + 10:2], T.ik[:, 1 - c:2 - c], A.add, A.add)
+    if r < 2: quant_w(3)
 
     def nio(q): return 11 if r == 1 or (r == 0 and q < 2) else 10
-    def ncs(s, q): return ne if q == (1 if s == 0 else (s + 3) % N) else h2
+    def ncs(s, q): return ne if q == (s + 3) % N else h2
     def block(t, k, q): return t[32 * k:32 * k + 32, 0:nio(q)]
-    def spread(q, out): return [S("act", [io], block(out, k, q), block(T.iof, q, q), F.Copy) for k in range(4)][-1]
-    def more(): return V("ts", [ae], T.iof[:, 10:11], T.ace[:], -0.5, PB + 255.0 + 8, A.mult, A.add)
-    if r == 1: io = more()
+    def made(q): return T.J[32 * q:32 * q + 32, L:L + nio(q)]
+    def spread(q, out): return [S("lin", [io], block(out, k, q), made(q), -1.0 / 128, 256.0) for k in range(4)][-1]
     pls, pss = [], []
-    to = [2, 3, 1] if r == 0 else [(r + dq) % N for dq in range(1, N)]
+    to = [(r + dq) % N for dq in range(1, N)]
     OF = [T["of%d" % at(q, r)][:, 0:nio(q)] for q in to]
     SP = [T["sp%d" % at(q, r)] for q in to]
-    z = [V("copy", [io], block(T["of%d" % at(to[0], r)], k, to[0]), block(T.iof, to[0], to[0])) for k in range(4)][-1:]
-    if r == 0: io2 = more()
-    for n in (1, 2):
-        if r == 0 and n == 2: io = io2
-        z.append(spread(to[n], SP[n]))
+    z = [V("ts", [io], block(T["of%d" % at(to[0], r)], k, to[0]), made(to[0]), -1.0 / 128, 256.0, A.mult, A.add) for k in range(4)][-1:]
+    for n in (1, 2): z.append(spread(to[n], SP[n]))
     for n, q in enumerate(to):
         i, j, nq = at(q, r), at(r, q), nio(q)
         wd = 168 if nq == 11 else 160
@@ -294,35 +299,28 @@ def rank_program(g, core, T, topo):
         pls.append(([q], eng[q][n * h2:n * h2 + h2] if n < 2 else eng[q], T.sem["cs%d" % j], T["pks%d" % i][:, 0:wd], [T.es[:, RG * r:RG * r + wd]]))
         if n == 2:
             wait("p", pss[1:2])
-            send(pls[:2])
+            if nio(to[0]) == nio(to[1]): send(pls[:2])
+            else:
+                for t in pls[:2]: send([t])
         wait("p", [pq])
         send([([q], eng[q], T.sem["cq%d" % j], U8(T["pkq%d" % i][:, 0:wd]), [U8(T.eq[:, RG * r:RG * r + wd])])])
     wait("p", pss[2:])
     send(pls[2:])
 
     z = spread(r, T.spo)
-    en = V("scan", [own] + inf[:r] + inf[r + 1:], T.en[:, 0:4], T.inf[:, 0:32:8], T.zb[:, 0:4], -0.5 * U, A.add, A.add)
-    x = V("tt", [en, r0s], T.en[:, 4:6], T.en[:, 0:2], T.r0[:, 8:17:8], A.add)
-    G = lambda c: T.g[:, 8 * c:8 * c + 8]
-    for n, c in ((4, 2), (5, 3), (0, 0), (2, 1), (1, 4), (3, 5)):
-        sg = S("sign", [x if c > 3 else en], G(n), T.nP[:], -1.0, T.en[:, c:c + 1])
-    ze = V("quant", [mz], T.eq[:, 4 * RG:4 * RG + 160], T.es[:, 4 * RG:4 * RG + 160], T.zt[:])
-    quant_w(0)
+    V("scan", inf[:r] + inf[r + 1:], T.thr[:, 0:8:2], T.inf[:, 63:256:64], T.zb[:, 0:4], 0.0, A.add, A.add)
+    V("ts", [], T.thr[:, 1:2], T.inf[:, 63:64], T.inf[:, 126:127], None, A.add)
+    x = V("ts", [], T.thr[:, 3:4], T.inf[:, 63:64], i1, T.inf[:, 190:191], A.add, A.add)
+    quant_w(4)
+    x = V("tt", [x, kS, ko], T.G[:], T.thr[:].indirect(T.o7[:]), T.nP[:], A.is_le)
     no = nio(r)
     y = V("copy", [z], T.ioo[:, 0:no], T.spo[:, 0:no])
+    quant_w(5)
+    x = V("scan", [x], T.Fo[:], T.G[:], T.W[:], 0.0, A.mult, A.add)
     off = T.ioo[:, 0:no]
     pe = V("copy", [y], U32(T.eq[:, RG * r:RG * r + 16 * no]), U32(T.padq[:]).indirect(off))
     pf = S("act", [y], T.es[:, RG * r:RG * r + 16 * no], T.pads[:].indirect(off), F.Copy)
-    y = V("tt", [sg], T.gb[:], G(4), G(5), A.add)
-    b = V("tt", [], T.gac[:], T.g[:, 0:16], T.g[:, 16:32], A.add)
-    x = V("tt", [y], T.gs[:], T.slot[:], T.gb[:], A.subtract)
-    b = V("tt", [b], T.bb[:], T.gac[:, 0:8], T.gac[:, 8:16], A.subtract) if r < 2 else V("tt", [b], T.bb[:], G(2), G(3), A.subtract)
-    V("tt", [x], T.b1[:], T.gs[:], T.gac[:, 8:16], A.subtract)
-    b = V("tt", [b], T.uu[:], T.bb[:], T.cE[:], A.mult)
-    V("tt", [], T.bf[:, 0:8], T.gs[:], T.gac[:, 0:8], A.subtract)
-    b = V("tt", [b], T.bf[:, 8:16], T.b1[:], T.uu[:], A.subtract)
-    fd = V("ts", [b], T.fo[:], T.bf[:], RG / 2.0, None, A.mult)
-    quant_w(1)
+    fd = V("copy", [x], T.fo[:], T.Fo[:, 7:128:8])
 
     cq = [("cq%d" % at(q, r), ne) for q in others]
     cs = [("cs%d" % at(q, r), ncs(q, r)) for q in others]
@@ -330,17 +328,17 @@ def rank_program(g, core, T, topo):
         lo, hi = 128 * n, 128 * n + 128
         s = slice(32 * k, 32 * k + 4 * RG + 32)
         off = T.fo[:, 8:16] if k == 3 else T.fo[:, 0:8]
-        if n in (2, 3): quant_w(n)
         a = V("copy", [pe, fd] + cq, U32(T.xfq[:, lo:hi]), U32(T.eq[:, s]).indirect(off))
+        if n < 4: quant_w(6 + n)
         b = S("act", [pf, fd, ze] + cs, T.xfs[:, lo:hi], T.es[:, s].indirect(off), F.Copy)
         ms = []
         for o in range(2):
             w = 128 * (2 * n + o)
-            ms.append(op("t", "mm", [a, b, qw[n]], T.yp[:, 512 * o:512 * o + 128],
+            ms.append(op("t", "mm", [a, b, qw[2 * n + o]], T.yp[:, 512 * o:512 * o + 128],
                          T.wq[:, w:w + 128], T.ws[:, w:w + 128], T.xfq[:, lo:hi], T.xfs[:, lo:hi], n == 0, n == 4))
     x = V("copy", [ms[0]], T.ys[:, 0:128], T.yp[:, 0:128])
     dma("s", "st0", [x], T.y[:, 0:128], T.ys[:, 0:128])
     x = S("act", [ms[1]], T.ys[:, 128:256], T.yp[:, 512:640], F.Copy)
     dma("a", "st1", [x], T.y[:, 128:256], T.ys[:, 128:256])
     wait("p", [(k, n) for k, n in cnt.items()])
-    wait("p", [hal, bdr, flg, r0s] + inf[:r] + inf[r + 1:])
+    wait("p", [hal, bdr, flg] + inf[:r] + inf[r + 1:])

@@ -6,7 +6,6 @@ F = ActivationFunctionType
 CODE = "float8_e4m3fn_x4"
 RG = 176
 M128 = 24576.0
-M32 = 6144.0
 YW = 300
 
 
@@ -23,16 +22,16 @@ SCRATCH = {
     "xfq": sb(640, CODE), "xfs": sb(640, "uint8"), "ys": sb(256),
     "sc": ("psum", [128, 1024], "float32"), "yp": ("psum", [128, 1024], "float32"),
     "pI": sb(1, I32), "pm": sb(4, I32), "pf": sb(4), "i16": sb(16), "i64": sb(2), "nI": sb(128), "nP": sb(128), "W": sb(128),
-    "b2": sb(1), "b3": sb(1), "na": sb(1), "ka": sb(1), "kb": sb(1), "tp": sb(2), "o7": sb(8, U16), "zb": sb(16, BF),
+    "b2": sb(1), "b3": sb(1), "na": sb(1), "ka": sb(1), "kb": sb(1), "tp": sb(32), "o7": sb(8, U16), "zb": sb(16, BF),
     "s": sb(276, BF), "s2": sb(256, BF), "B": sb(64, BF), "BT": sb(64, BF), "H": sb(274, BF), "A2": sb(256, BF), "T2": sb(256, BF),
     "TT": sb(64, BF), "fa": sb(256, BF), "fb": sb(256, BF), "Si": sb(256, BF), "S": sb(288, BF), "EL": sb(64, BF), "eb": sb(64, BF),
-    "bd": sb(16, BF), "fl": sb(8, BF), "inf": sb(256), "ini": sb(2), "th2": sb(1, BF), "E1": sb(1), "ik": sb(2), "ike": sb(1), "RB": sb(32, BF), "R16": sb(32, BF), "Sl": sb(16, BF),
-    "D": sb(2), "K": sb(2, BF), "De": sb(1), "Ke": sb(1, BF), "Y": sb(2 * YW, BF), "Ye": sb(16, BF), "J": sb(YW, BF),
-    "thr": sb(8), "G": sb(128), "Fo": sb(128), "fo": sb(16, U16), "ioo": sb(12, U16), "spo": sb(12),
+    "bd": sb(16, BF), "fl": sb(8, BF), "inf": sb(256), "th2": sb(1, BF), "E1": sb(1), "ik": sb(2), "ike": sb(1),
+    "RB": sb(32, BF), "R16": sb(32, BF), "Sl": sb(16),
+    "D": sb(2), "K": sb(2, BF), "Ke": sb(1, BF), "Y": sb(2 * YW, BF), "Ye": sb(16, BF), "J": sb(YW, BF),
+    "thr": sb(8), "G": sb(128), "Fo": sb(128), "fo": sb(16, U16), "ioo": sb(12, U16), "spo": sb(12), "sp": sb(12),
 }
 for _i in range(3):
     SCRATCH["of%d" % _i] = sb(12, U16)
-    SCRATCH["sp%d" % _i] = sb(12)
     SCRATCH["pkq%d" % _i] = sb(RG, CODE)
     SCRATCH["pks%d" % _i] = sb(RG, "uint8")
 SEMAPHORES = ["vc", "ac", "tc", "pc", "ldu", "ldxa", "ldxb", "ldw0", "ldw1", "ldw2", "ldw3", "ldw4", "halo", "bdr", "inf0", "inf1", "inf2", "inf3",
@@ -106,10 +105,18 @@ def rank_program(g, core, T, topo):
     ex_out, ex_in = r in (0, 1), r in (1, 2)
     PB = 128 if dn else 129
     L = 288 if r == 0 else 272
+    ldw, qw = {}, {}
+
+    def load_w(k, deps): ldw[k] = dma("s", "ldw%d" % k, deps, T.wt[:, 1024 * k:1024 * k + 1024], T.w[:, 1024 * k:1024 * k + 1024])
+
+    def quant_w(m=1):
+        for n in range(len(qw), min(10, len(qw) + m)):
+            qw[n] = V("quant", [ldw[n // 2]], T.wq[:, 128 * n:128 * n + 128], T.ws[:, 128 * n:128 * n + 128], T.wt[:, 512 * n:512 * n + 512])
     ldu = dma("a", "ldu", [], T.ut[:], T.u[:, 0:8])
     dma("s", "ldxa", [], T.xt[:, 256:512], T.x[:, 0:256])
     ldxa = dma("a", "ldxa", [], T.xt[:, 0:256], T.x[:, 768:1024])
     ldxb = dma("s", "ldxb", [], T.xt[:, 512:1024], T.x[:, 256:768])
+    for k in (0, 1, 2, 3, 4): load_w(k, [])
     kp = op("p", "iota", [], T.pI[:], [[0, 1]], 0, 1)
     op("p", "iotaf", [], T.i16[:], [[0, 8], [16, 2]], 0, 0)
     if r == 0: op("p", "iotaf", [], T.i64[:], [[64, 2]], -64, 0)
@@ -125,6 +132,7 @@ def rank_program(g, core, T, topo):
     V("memset", [], T.zb[:], 0.0)
     kf = V("copy", [k], T.pf[:], T.pm[:])
     ze = V("quant", [], T.eq[:, 4 * RG:4 * RG + 160], T.es[:, 4 * RG:4 * RG + 160], T.zt[:])
+    if r == 0: k0 = V("memset", [], T.tp[:], 0.0)
 
     for t in range(4): k = V("ts", [ldu], T.ur[:, t:512:4], T.zt[:, 0:128], T.ut[:, t:t + 1], None, A.add)
     if dn: V("quant", [], T.padq[:, 416:544], T.pads[:, 416:544], T.zt[:, 0:512])
@@ -136,191 +144,207 @@ def rank_program(g, core, T, topo):
         qx[h] = V("quant", [ld], T.xq[:, c], T.xs[:, c], T.xt[:, 512 * h:512 * h + 512])
         mm[h] = op("t", "mm", [qu, qx[h]], T.sc[:, 512 * h:512 * h + 128], T.urq[:], T.urs[:], T.xq[:, c], T.xs[:, c], True, True)
     score(0, ldxa)
-    k = V("memset", [], T.Y[:, L:L + 10], 0.0)
-    k = V("memset", [], T.Y[:, YW + L:YW + L + 10], 0.0)
+    V("memset", [], T.Y[:, L:L + 10], 0.0)
+    V("memset", [], T.Y[:, YW + L:YW + L + 10], 0.0)
     V("memset", [], T.thr[:, 5:6], 0.0)
-    V("memset", [], T.thr[:, 7:8], 1e9)
     score(1, ldxb)
-    ldw, qw = {}, {}
-
-    def load_w(k, deps): ldw[k] = dma("s", "ldw%d" % k, deps, T.wt[:, 1024 * k:1024 * k + 1024], T.w[:, 1024 * k:1024 * k + 1024])
-    def quant_w(n): qw[n] = V("quant", [ldw[n // 2]], T.wq[:, 128 * n:128 * n + 128], T.ws[:, 128 * n:128 * n + 128], T.wt[:, 512 * n:512 * n + 512])
-    load_w(0, [ldxb])
+    V("memset", [], T.thr[:, 7:8], 1e9)
+    ko = V("ts", [], T.o7[:], T.zb[:, 0:8], T.pf[:, 1:2], 7.0, A.subtract, A.add)
+    xz = [T.xp[:, (192 if dn else 0) + t:1216 if dn else 1088:68] for t in range(4)] + [T.xp[:, 0:128] if dn else T.xp[:, 1088:1216]]
+    V("memset", [], xz[0], 0.0)
 
     nb = ([(r - 1, 64, 400)] if up else []) + ([(r + 1, 48, 112)] if r == N - 2 else [])
 
+    def share(q, n, m): return eng[q][n * ne // m:(n + 1) * ne // m]
+
     def strips(view):
         if nb:
-            send([([q], eng[q][n * h2:n * h2 + h2], T.sem.halo, view("xq", "xs", src), [view("padq", "pads", dst)]) for n, (q, src, dst) in enumerate(nb)])
+            send([([q], share(q, n, len(nb)), T.sem.halo, view("xq", "xs", src), [view("padq", "pads", dst)]) for n, (q, src, dst) in enumerate(nb)])
     wait("p", [qx[0]])
     strips(lambda q, s, a: U8(T[q][:, a:a + 16]))
-    hal = ("halo", 2 * h2)
+    hal = ("halo", 2 * (h2 if r in (1, 3) else ne))
 
-    if r == 0:
-        k = S("lin", [kf, kg], T.b2[:], T.pf[:, 2:3], 32.0, T.pf[:, 1:2])
-        k = S("lin", [k], T.b3[:], T.pf[:, 3:4], 8.0, T.b2[:])
-        k = S("lin", [k], T.b2[:], T.b3[:], -1.0, M128 + 63.5)
-        k = S("lin", [k], T.tp[:], T.i64[:], 1.0, T.b2[:])
-        kt = S("lin", [k], T.K[:], T.tp[:], 1.0, 0.0)
-    S("lin", [kf, kg], T.na[:], T.pf[:, 3:4], -8.0, M128 + 63.5)
+    S("lin", [kf], T.na[:], T.pf[:, 3:4], -8.0, M128 + 63.5)
+    if r == 0: S("lin", [], T.b2[:], T.pf[:, 2:3], 32.0, T.pf[:, 1:2])
     S("lin", [], T.ka[:], T.pf[:, 2:3], 8.0, RG - 64.0)
     k = S("lin", [], T.kb[:], T.pf[:, 2:3], -8.0, 64.0)
-    S("lin", [], T.W[:, 7:128:8], T.i16[:], 1.0, T.pf[:, 0:1])
+    S("lin", [kg], T.W[:, 7:128:8], T.i16[:], 1.0, T.pf[:, 0:1])
+    if r == 0: kt = S("lin", [k], T.b3[:], T.b2[:], -1.0, T.na[:])
     S("lin", [k], T.nP[:], T.nI[:], 1.0, T.na[:])
     for j in (3, 5):
         plain = j == 5 and r >= 2
         S("lin", [], T.W[:, 64 + j:128:8], T.i16[:, 0:8], 0.0 if plain else 1.0, float(RG) if plain else T.ka[:])
         kS = S("lin", [], T.W[:, 65 + j:128:8], T.i16[:, 0:8], 0.0 if plain else -1.0, 0.0 if plain else T.kb[:])
+    if r == 0: kt = S("lin", [kt, k0], T.tp[:, 0:32:16], T.i64[:], 1.0, T.b3[:])
     xp0 = 128 if dn else 4
-    for i in range(16):
-        a = 64 * ((i + 4) % 16)
-        kX = S("act", [ldxa, ldxb], T.xp[:, xp0 + 68 * i:xp0 + 68 * i + 64], T.xt[:, a:a + 64], F.Copy)
+
+    def rows(lo, hi):
+        for i in range(lo, hi):
+            a = 64 * ((i + 4) % 16)
+            k = S("act", [ldxa, ldxb], T.xp[:, xp0 + 68 * i:xp0 + 68 * i + 64], T.xt[:, a:a + 64], F.Copy)
+        return k
+    rows(0, 8)
 
     V("ts", [mm[0]], T.B[:, 0:32], T.sc[:, 48:80], 1.0 / 32, -1.0 / 32, A.min, A.max)
     kb = V("ts", [], T.B[:, 32:64], T.sc[:, 48:80], 6.25 / 32, -9.75 / 32, A.min, A.max)
 
     def signs(out, a, b, k, deps): return V("ts", deps, out, T.sc[:, a:b], 0.0, k, A.is_gt, A.add)
-    signs(T.s[:, 3:19], 64, 80, -0.5, [])
     signs(T.s[:, 19:83], 64, 128, -0.5, [])
-    signs(T.s[:, 211:275], 0, 64, -0.5, [])
+    k = signs(T.s[:, 211:275], 0, 64, -0.5, [])
     kb = V("turn", [kb], T.BT[:], T.B[:])
-    signs(T.s2[:, 0:48], 80, 128, 7.5, [])
-    signs(T.s2[:, 176:240], 0, 64, 7.5, [])
-    signs(T.s2[:, 240:256], 48, 64, 7.5, [])
-    signs(T.s[:, 83:211], 512, 640, -0.5, [mm[1]])
-    p = signs(T.s2[:, 48:176], 512, 640, 7.5, [])
+    sd = S("lin", [k], T.s[:, 3:19], T.s[:, 19:35], 1.0, 0.0)
+    for a, b, c in ((0, 48, 35), (176, 240, 211), (240, 256, 259)): s2 = S("lin", [], T.s2[:, a:b], T.s[:, c:c + b - a], 1.0, 8.0)
+    kX = rows(8, 16)
+    p = signs(T.s[:, 83:211], 512, 640, -0.5, [mm[1]])
+    p2 = signs(T.s2[:, 48:176], 512, 640, 7.5, [])
     wait("p", [kb])
-    send(([([r - 1], eng[r - 1][:h2], T.sem.bdr, T.BT[:, 31:33], [T.bd[:, 8:10]])] if up else [])
-         + ([([r + 1], eng[r + 1][h2:], T.sem.bdr, T.BT[:, 31:33], [T.bd[:, 0:2]])] if dn else []))
+    nbr = [q for q in (r - 1, r + 1) if 0 <= q < N]
+    send([([q], share(q, n, len(nbr)), T.sem.bdr, T.BT[:, 31:33], [T.bd[:, 8:10] if q < r else T.bd[:, 0:2]]) for n, q in enumerate(nbr)])
     strips(lambda q, s, a: T[s][:, a:a + 16])
-    for j, d in ((1, -1.0), (3, 1.0), (7, -18.0)): V("memset", [], T.Y[:, L + j:2 * YW:YW], -128 * d)
+    bdr = ("bdr", sum(ne if q in (0, N - 1) else h2 for q in nbr))
+    V("memset", [], xz[1], 0.0)
 
-    k = V("scan", [p], T.H[:, 0:273], T.s[:, 3:276], T.s[:, 0:273], 0.0, A.add, A.subtract)
-    V("scan", [], T.A2[:], T.s[:, 3:259], T.s2[:], 100.0, A.min, A.add)
+    k = V("scan", [p, sd], T.H[:, 0:273], T.s[:, 3:276], T.s[:, 0:273], 0.0, A.add, A.subtract)
+    V("scan", [p2, s2], T.A2[:], T.s[:, 3:259], T.s2[:], 100.0, A.min, A.add)
     V("tt", [k], T.H[:, 17:273:16], T.s[:, 19:275:16], T.s[:, 20:276:16], A.add)
     k = V("tt", [], T.H[:, 32:273:16], T.s[:, 33:275:16], T.s[:, 34:275:16], A.add)
-    for j, d in ((5, 1.0), (9, 34.0)): V("memset", [], T.Y[:, L + j:2 * YW:YW], -128 * d)
-    ko = V("ts", [], T.o7[:], T.zb[:, 0:8], T.pf[:, 1:2], 7.0, A.subtract, A.add)
+    for j, d in ((1, -1.0), (3, 1.0), (7, -18.0)): V("memset", [], T.Y[:, L + j:2 * YW:YW], -128 * d)
     k = V("scan", [k], T.T2[:], T.H[:, 17:273], T.A2[:], 100.0, A.min, A.add)
-    load_w(1, [k])
-    for t in range(3): V("memset", [], T.xp[:, (192 if dn else 0) + t:1216 if dn else 1088:68], 0.0)
+    for j, d in ((5, 1.0), (9, 34.0)): V("memset", [], T.Y[:, L + j:2 * YW:YW], -128 * d)
+    V("memset", [], xz[2], 0.0)
     if up: tt = V("turn", [k], T.TT[:, 32:64], T.T2[:, 0:32])
     if ex_in:
         wait("p", [tt])
-        send([([r - 1], e0[:h2], T.sem.flg, T.TT[:, 32:33], [T.fl[:, 0:1]])])
+        send([([r - 1], e0, T.sem.flg, T.TT[:, 32:33], [T.fl[:, 0:1]])])
     if dn: tt = V("turn", [k], T.TT[:, 0:32], T.T2[:, 224:256])
     V("ts", [], T.fa[:], T.T2[:], 6.25, None, A.is_gt)
     k = V("ts", [], T.fb[:], T.T2[:], 9.75, None, A.is_gt)
 
-    bdr = ("bdr", h2 * len([q for q in (r - 1, r + 1) if 0 <= q < N]))
     a, b = (0 if dn else 32), (64 if up else 32)
     if dn: x = V("ts", [bdr, tt], T.EL[:, 0:32], T.TT[:, 0:32], T.bd[:, 8:9], T.bd[:, 9:10], A.mult, A.is_le)
     if up: x = V("ts", [bdr, tt], T.EL[:, 32:64], T.TT[:, 32:64], T.bd[:, 0:1], T.bd[:, 1:2], A.mult, A.is_le)
     si = V("scan", [k], T.Si[:], T.fa[:], T.fb[:], 0.0, A.add, A.subtract)
     x = V("turn", [x], T.eb[:, a:b], T.EL[:, a:b])
     x15, x0, c0 = T.eb[:, 16:32], T.eb[:, 32:48], 64 * r
-    V("memset", [], T.xp[:, (192 if dn else 0) + 3:1216 if dn else 1088:68], 0.0)
-    mp = V("memset", [], T.xp[:, 0:128] if dn else T.xp[:, 1088:1216], 0.0)
+    V("memset", [], xz[3], 0.0)
+    mp = V("memset", [], xz[4], 0.0)
     if r == 0:
-        k = V("ts", [si, kt], T.ini[:], T.tp[:], T.Si[:, 255:256], None, A.add)
-        for c in (0, 1): own = V("scan", [x, k], T.inf[:, 32 + c:64:2], x15, T.zb[:], T.ini[:, c:c + 1], A.add, A.add)
+        for c in (0, 1): own = V("scan", [x, si, kt], T.inf[:, 32 + c:64:2], x15, T.tp[:, 16 * c:16 * c + 16], T.Si[:, 255:256], A.add, A.add)
     else:
         if dn: V("scan", [x, si], T.inf[:, c0 + 32:c0 + 64:2], x0, T.zb[:], T.Si[:, 15:16], A.add, A.add)
         own = V("scan", [x, si], T.inf[:, c0 + 33:c0 + 64:2], x0, x15 if dn else T.zb[:], T.Si[:, 255:256], A.add, A.add)
     wait("p", [own])
     msg = T.inf[:, c0 + (62 if dn else 63):c0 + 64]
-    send([(others[::-1], e0, T.sem["inf%d" % r], msg, [msg] * 3)])
+    send([([1, 3, 2] if r == 0 else others[::-1], e0, T.sem["inf%d" % r], msg, [msg] * 3)])
     inf = [("inf%d" % q, ne) for q in range(N)]
-    flg = ("flg", h2) if ex_out else None
+    flg = ("flg", ne) if ex_out else None
 
     if up: k = V("tt", [], T.fa[:, 0:16], T.fa[:, 0:16], x0, A.add)
     if dn: k = V("tt", [], T.fa[:, 240:256], T.fa[:, 240:256], x15, A.add)
-    load_w(2, [k])
     if ex_out:
         x = S("lin", [kb], T.th2[:], T.BT[:, 32:33], 1.0, 3.5 / 32)
         x = V("ts", [flg, x], T.RB[:], T.BT[:, 0:32], T.fl[:, 0:1], T.th2[:], A.mult, A.is_lt)
-    quant_w(0)
-    k = V("scan", [k], T.S[:, 0:256], T.fa[:], T.fb[:], 0.0, A.add, A.subtract)
-    te = M128 + 62 - 4 * (M128 + 63.5)
+    te = (M128 + 62) / 4 - M128 - 63.5
     if r == 0: E1 = V("memset", [], T.E1[:], te)
-    if r == 1: E1 = V("ts", [own], T.E1[:], T.inf[:, 127:128], 4.0, te, A.mult, A.add)
+    if r == 1: E1 = V("ts", [own], T.E1[:], T.inf[:, 127:128], te, None, A.add)
+    if not ex_out: quant_w()
+    k = V("scan", [k], T.S[:, 0:256], T.fa[:], T.fb[:], 0.0, A.add, A.subtract)
     if ex_out: x = V("turn", [x], T.R16[:], T.RB[:])
-    quant_w(1)
-    sp = V("copy", [k], T.S[:, 256:272], T.S[:, 15:256:16])
-    if r == 0: sp = V("scan", [x], T.S[:, 272:288], T.R16[:, 0:16], T.zb[:], T.S[:, 255:256], A.add, A.add)
-    if ex_out: sp = V("scan", [x], T.Sl[:], T.R16[:, 0:16], T.zb[:], 0.0, A.add, A.add)
     a = 96 if dn else 128
     pp = V("quant", [kX, mp], T.padq[:, a:a + 304], T.pads[:, a:a + 304], T.xp[:])
-    for k in (3, 4): load_w(k, [pp])
+    sp = V("copy", [k], T.S[:, 256:272], T.S[:, 15:256:16])
+    if r == 0: sp = V("scan", [x], T.S[:, 272:288], T.R16[:, 0:16], T.zb[:], T.S[:, 255:256], A.add, A.add)
+    if ex_out: sp = V("scan", [x, E1], T.Sl[:], T.R16[:, 0:16], T.zb[:], T.E1[:], A.add, A.add)
+    quant_w((0, 1, 2, 2)[r])
 
     i0, i1, i2 = T.inf[:, 62:64], T.inf[:, 127:128], T.inf[:, 191:192]
-    d0, m = (63 if r == 1 else 1), None
-    if r == 1: m = V("copy", inf[:1], T.K[:], i0)
-    for out in (T.K, T.D):
-        if r == 2: m = V("ts", inf[:2], out[:], i0, i1, None, A.add)
-        if r == 3: m = V("ts", inf[:3], out[:], i0, i1, i2, A.add, A.add)
-    for out in (T.Ke, T.De):
-        if ex_out: m = V("ts", [E1], out[:], T.inf[:, 63:64], 4.0, T.E1[:], A.mult, A.add)
-    if r > 1: quant_w(2)
-    def rounded(c): return V("ts", [sp, m if r > 1 else None], T.Y[:, YW * c:YW * c + L], T.S[:, 0:L], (T.tp, T.inf, T.D, T.D)[r][:, d0 - c:d0 - c + 1],
-                             M128 + (128 if r == 0 else 1024), A.add, A.min)
-    rounded(1)
-    V("ts", [m], T.ik[:], T.K[:], -float(L), -128.0 * (PB - 256 + L), A.mult, A.add)
-    if ex_out:
-        V("ts", [], T.Ye[:], T.Sl[:], 4.0, T.De[:], A.mult, A.add)
-        x = V("ts", [], T.ike[:], T.Ke[:], -16.0, -128.0 * (PB + 15), A.mult, A.add)
-    y = rounded(0)
-    if ex_out: y = V("scan", [x], T.J[:, L - 4:L + 11:2], T.Ye[:, 0:16:2], T.Ye[:, 1:16:2], T.ike[:], A.add, A.add)
-    if r < 2: quant_w(2)
-    else: quant_w(3)
-    for c in (1, 0):
+
+    def rounded(c, deps):
+        out, a = T.Y[:, YW * c:YW * c + L], T.S[:, 0:L]
+        if r == 0: return V("ts", deps, out, a, T.tp[:, 16 - 16 * c:17 - 16 * c], M128 + 128, A.add, A.min)
+        if r == 2: return V("ts", deps, out, a, T.inf[:, 63 - c:64 - c], i1, A.add, A.add)
+        return V("ts", deps, out, a, T.inf[:, 63 - c:64 - c] if r == 1 else T.D[:, 1 - c:2 - c], None, A.add)
+
+    def start(deps): return V("ts", deps, T.ik[:], T.K[:], -float(L), -128.0 * (PB - 256 + L), A.mult, A.add)
+
+    def count(c, deps):
         a = YW * c
-        io = V("scan", [y], T.J[:, c:L + 10:2], T.Y[:, a:a + L + 10:2], T.Y[:, a + 1:a + L + 10:2], T.ik[:, 1 - c:2 - c], A.add, A.add)
-    if r < 2: quant_w(3)
+        return V("scan", deps, T.J[:, c:L + 10:2], T.Y[:, a:a + L + 10:2], T.Y[:, a + 1:a + L + 10:2], T.ik[:, 1 - c:2 - c], A.add, A.add)
+
+    def ends(n):
+        if n == 0: return V("scan", inf[:r] + inf[r + 1:], T.thr[:, 0:8:2], T.inf[:, 63:256:64], T.zb[:, 0:4], 0.0, A.add, A.add)
+        if n == 1: return V("ts", [], T.thr[:, 1:2], T.inf[:, 63:64], T.inf[:, 126:127], None, A.add)
+        return V("ts", [], T.thr[:, 3:4], T.inf[:, 63:64], i1, T.inf[:, 190:191], A.add, A.add)
+
+    def passed(deps): return V("tt", deps + [kS, ko], T.G[:], T.thr[:].indirect(T.o7[:]), T.nP[:], A.is_le)
+    if ex_out:
+        x = V("ts", [E1] + inf[:r], T.Ke[:], T.inf[:, 63:64], T.E1[:], 4.0, A.add, A.mult)
+        if r == 1: k = V("copy", [], T.K[:], i0)
+        V("ts", [sp], T.Ye[:], T.Sl[:], T.inf[:, 63:64], 4.0, A.add, A.mult)
+        rounded(1, [])
+        x = V("ts", [x], T.ike[:], T.Ke[:], -16.0, -128.0 * (PB + 15), A.mult, A.add)
+        k = start([k]) if r == 1 else V("memset", [], T.ik[:], -L * M128 - 128.0 * (PB - 256 + L))
+        y = rounded(0, [])
+        x = V("scan", [x], T.J[:, L - 4:L + 11:2], T.Ye[:, 0:16:2], T.Ye[:, 1:16:2], T.ike[:], A.add, A.add)
+        count(1, [k])
+        quant_w()
+        io = count(0, [x])
+    elif r == 2:
+        k = V("ts", inf[:2], T.K[:], i0, i1, None, A.add)
+        for c in (1, 0): rounded(c, [sp])
+        k = start([k])
+        quant_w()
+        for c in (1, 0): io = count(c, [k])
+    else:
+        x = V("ts", inf[:3], T.D[:], i0, i1, i2, A.add, A.add)
+        k = V("ts", [], T.K[:], i0, i1, i2, A.add, A.add)
+        quant_w()
+        rounded(1, [sp, x])
+        k = start([k])
+        y = rounded(0, [])
+        count(1, [k])
+        io = count(0, [y])
+    quant_w()
 
     def nio(q): return 11 if r == 1 or (r == 0 and q < 2) else 10
-    def ncs(s, q): return ne if q == (s + 3) % N else h2
+    def ncs(s, q): return ne if q == (s + 3) % N or s == 0 else h2
     def block(t, k, q): return t[32 * k:32 * k + 32, 0:nio(q)]
     def made(q): return T.J[32 * q:32 * q + 32, L:L + nio(q)]
     def spread(q, out): return [S("lin", [io], block(out, k, q), made(q), -1.0 / 128, 256.0) for k in range(4)][-1]
-    pls, pss = [], []
+    pls, pqs, pss = [], [], []
     to = [(r + dq) % N for dq in range(1, N)]
-    OF = [T["of%d" % at(q, r)][:, 0:nio(q)] for q in to]
-    SP = [T["sp%d" % at(q, r)] for q in to]
-    z = [V("ts", [io], block(T["of%d" % at(to[0], r)], k, to[0]), made(to[0]), -1.0 / 128, 256.0, A.mult, A.add) for k in range(4)][-1:]
-    for n in (1, 2): z.append(spread(to[n], SP[n]))
+    OF = [T["of%d" % at(q, r)] for q in to]
+    z = [[V("ts", [io], block(OF[n], k, to[n]), made(to[n]), -1.0 / 128, 256.0, A.mult, A.add) for k in range(4)][-1] for n in (0, 1)]
+    z.append(spread(to[2], T.sp))
     for n, q in enumerate(to):
         i, j, nq = at(q, r), at(r, q), nio(q)
         wd = 168 if nq == 11 else 160
-        pq = V("copy", [z[n], pp, hal], U32(T["pkq%d" % i][:, 0:16 * nq]), U32(T.padq[:]).indirect(OF[n]))
-        if n == 0:
-            for o in (1, 2): z[o] = V("copy", [z[o]], OF[o], SP[o][:, 0:nio(to[o])])
-        pss.append(S("act", [z[n], pp, hal], T["pks%d" % i][:, 0:16 * nq], T.pads[:].indirect(OF[n]), F.Copy))
-        pls.append(([q], eng[q][n * h2:n * h2 + h2] if n < 2 else eng[q], T.sem["cs%d" % j], T["pks%d" % i][:, 0:wd], [T.es[:, RG * r:RG * r + wd]]))
-        if n == 2:
-            wait("p", pss[1:2])
-            if nio(to[0]) == nio(to[1]): send(pls[:2])
-            else:
-                for t in pls[:2]: send([t])
-        wait("p", [pq])
-        send([([q], eng[q], T.sem["cq%d" % j], U8(T["pkq%d" % i][:, 0:wd]), [U8(T.eq[:, RG * r:RG * r + wd])])])
-    wait("p", pss[2:])
-    send(pls[2:])
+        pq = V("copy", [z[n], pp, hal], U32(T["pkq%d" % i][:, 0:16 * nq]), U32(T.padq[:]).indirect(OF[n][:, 0:nq]))
+        if n == 0: z[2] = V("copy", [z[2]], OF[2][:, 0:nio(to[2])], T.sp[:, 0:nio(to[2])])
+        pss.append(S("act", [z[n], pp, hal], T["pks%d" % i][:, 0:16 * nq], T.pads[:].indirect(OF[n][:, 0:nq]), F.Copy))
+        pls.append(([q], eng[q][n * h2:n * h2 + h2] if ncs(r, q) == h2 else eng[q], T.sem["cs%d" % j], T["pks%d" % i][:, 0:wd], [T.es[:, RG * r:RG * r + wd]]))
+        pqs.append((pq, ([q], eng[q], T.sem["cq%d" % j], U8(T["pkq%d" % i][:, 0:wd]), [U8(T.eq[:, RG * r:RG * r + wd])])))
+    for kind, n in (("q", 0), ("s", 1), ("q", 1), ("s", 2), ("q", 2)):
+        wait("p", [pqs[n][0] if kind == "q" else pss[n]])
+        if kind == "q": send([pqs[n][1]])
+        elif n == 2: send(pls[2:])
+        elif r > 0: send(pls[:2])
+        else:
+            for t in pls[:2]: send([t])
 
     z = spread(r, T.spo)
-    V("scan", inf[:r] + inf[r + 1:], T.thr[:, 0:8:2], T.inf[:, 63:256:64], T.zb[:, 0:4], 0.0, A.add, A.add)
-    V("ts", [], T.thr[:, 1:2], T.inf[:, 63:64], T.inf[:, 126:127], None, A.add)
-    x = V("ts", [], T.thr[:, 3:4], T.inf[:, 63:64], i1, T.inf[:, 190:191], A.add, A.add)
-    quant_w(4)
-    x = V("tt", [x, kS, ko], T.G[:], T.thr[:].indirect(T.o7[:]), T.nP[:], A.is_le)
+    for n in range(3): th = ends(n)
+    quant_w()
+    x = passed([th])
     no = nio(r)
     y = V("copy", [z], T.ioo[:, 0:no], T.spo[:, 0:no])
-    quant_w(5)
+    quant_w()
     x = V("scan", [x], T.Fo[:], T.G[:], T.W[:], 0.0, A.mult, A.add)
     off = T.ioo[:, 0:no]
     pe = V("copy", [y], U32(T.eq[:, RG * r:RG * r + 16 * no]), U32(T.padq[:]).indirect(off))
     pf = S("act", [y], T.es[:, RG * r:RG * r + 16 * no], T.pads[:].indirect(off), F.Copy)
     fd = V("copy", [x], T.fo[:], T.Fo[:, 7:128:8])
+    quant_w((5, 3, 2, 2)[r])
 
     cq = [("cq%d" % at(q, r), ne) for q in others]
     cs = [("cs%d" % at(q, r), ncs(q, r)) for q in others]
@@ -329,7 +353,7 @@ def rank_program(g, core, T, topo):
         s = slice(32 * k, 32 * k + 4 * RG + 32)
         off = T.fo[:, 8:16] if k == 3 else T.fo[:, 0:8]
         a = V("copy", [pe, fd] + cq, U32(T.xfq[:, lo:hi]), U32(T.eq[:, s]).indirect(off))
-        if n < 4: quant_w(6 + n)
+        quant_w()
         b = S("act", [pf, fd, ze] + cs, T.xfs[:, lo:hi], T.es[:, s].indirect(off), F.Copy)
         ms = []
         for o in range(2):

@@ -21,21 +21,21 @@ SCRATCH = {
     "eq": sb(4 * RG + 160, CODE), "es": sb(4 * RG + 160, "uint8"),
     "xfq": sb(640, CODE), "xfs": sb(640, "uint8"), "ys": sb(256),
     "sc": ("psum", [128, 1024], "float32"), "yp": ("psum", [128, 1024], "float32"),
-    "pI": sb(1, I32), "pm": sb(4, I32), "pf": sb(4), "i16": sb(16), "i64": sb(2), "nI": sb(128), "nP": sb(128), "W": sb(128),
-    "b2": sb(1), "b3": sb(1), "na": sb(1), "ka": sb(1), "kb": sb(1), "tp": sb(32), "o7": sb(8, U16), "zb": sb(16, BF),
-    "s": sb(276, BF), "s2": sb(256, BF), "B": sb(64, BF), "BT": sb(64, BF), "H": sb(274, BF), "A2": sb(256, BF), "T2": sb(256, BF),
+    "pI": sb(1, I32), "pm": sb(4, I32), "pf": sb(4), "i16": sb(16), "i64": sb(2), "nI": sb(64), "nP": sb(64), "W": sb(128),
+    "b2": sb(1), "b3": sb(1), "na": sb(1), "ka": sb(1), "kb": sb(1), "tp": sb(32), "o7": sb(4, U16), "zb": sb(16, BF),
+    "s": sb(276, BF), "s2": sb(256, BF), "B": sb(32, BF), "BT": sb(32, BF), "H": sb(274, BF), "A2": sb(256, BF), "T2": sb(256, BF),
     "TT": sb(64, BF), "fa": sb(256, BF), "fb": sb(256, BF), "Si": sb(256, BF), "S": sb(288, BF), "EL": sb(64, BF), "eb": sb(64, BF),
-    "bd": sb(16, BF), "fl": sb(8, BF), "inf": sb(256), "th2": sb(1, BF), "E1": sb(1), "ik": sb(2), "ike": sb(1),
+    "bd": sb(16, BF), "BF": sb(32), "bf": sb(4), "TI": sb(32, I32), "fl": sb(8, BF), "inf": sb(256), "E1": sb(2), "ik": sb(2), "ike": sb(1),
     "RB": sb(32, BF), "R16": sb(32, BF), "Sl": sb(16),
-    "D": sb(2), "K": sb(2, BF), "Ke": sb(1, BF), "Y": sb(2 * YW, BF), "Ye": sb(16, BF), "J": sb(YW, BF),
-    "thr": sb(8), "G": sb(128), "Fo": sb(128), "fo": sb(16, U16), "ioo": sb(12, U16), "spo": sb(12), "sp": sb(12),
+    "D": sb(2), "K": sb(2, BF), "Ke": sb(1, BF), "Y": sb(2 * YW, BF), "Ye": sb(16, BF), "J": sb(320, BF),
+    "thr": sb(8), "G": sb(64), "Fo": sb(128), "fo": sb(16, U16), "ioo": sb(12, U16), "spo": sb(12), "sp": sb(12),
 }
 for _i in range(3):
     SCRATCH["of%d" % _i] = sb(12, U16)
     SCRATCH["pkq%d" % _i] = sb(RG, CODE)
     SCRATCH["pks%d" % _i] = sb(RG, "uint8")
-SEMAPHORES = ["vc", "ac", "tc", "pc", "ldu", "ldxa", "ldxb", "ldw0", "ldw1", "ldw2", "ldw3", "ldw4", "halo", "bdr", "inf0", "inf1", "inf2", "inf3",
-              "flg", "cq0", "cq1", "cq2", "cs0", "cs1", "cs2", "sent", "st0", "st1"]
+SEMAPHORES = ["vc", "ac", "tc", "pc", "ldu", "ldxa", "ldxb", "ldw0", "ldw1", "ldw2", "ldw3", "ldw4", "halo", "bd0", "bd1", "bd2", "bd3", "inf0", "inf1", "inf2", "inf3",
+              "flg", "r01", "cq0", "cq1", "cq2", "cs0", "cs1", "cs2", "sent", "st0", "st1"]
 
 
 def rank_program(g, core, T, topo):
@@ -116,53 +116,44 @@ def rank_program(g, core, T, topo):
     dma("s", "ldxa", [], T.xt[:, 256:512], T.x[:, 0:256])
     ldxa = dma("a", "ldxa", [], T.xt[:, 0:256], T.x[:, 768:1024])
     ldxb = dma("s", "ldxb", [], T.xt[:, 512:1024], T.x[:, 256:768])
-    for k in (0, 1, 2, 3, 4): load_w(k, [])
+    for k in range(5): load_w(k, [])
     kp = op("p", "iota", [], T.pI[:], [[0, 1]], 0, 1)
     op("p", "iotaf", [], T.i16[:], [[0, 8], [16, 2]], 0, 0)
     if r == 0: op("p", "iotaf", [], T.i64[:], [[64, 2]], -64, 0)
     op("p", "iotaf", [], T.W[:], [[0, 64], [-RG, 2]], RG, 0)
-    kg = op("p", "iotaf", [], T.nI[:], [[0, 2], [64, 8], [0, 8]], 8 * r, 0)
+    kg = op("p", "iotaf", [], T.nI[:], [[64, 8], [0, 8]], 8 * r, 0)
+    for t in range(4): kz = op("p", "iotaf", [], T.xp[:, (192 if dn else 0) + t:1216 if dn else 1088:68], [[0, 16]], 0, 0)
     mz = V("memset", [], T.zt[:], 0.0)
     V("ts", [kp], T.pm[:, 3:4], T.pI[:], 5, None, A.logical_shift_right)
     V("ts", [], T.pm[:, 0:1], T.pI[:], 15, None, A.bitwise_and)
     V("ts", [], T.pm[:, 1:2], T.pI[:], 7, None, A.bitwise_and)
     k = V("ts", [], T.pm[:, 2:3], T.pI[:], 3, 1, A.logical_shift_right, A.bitwise_and)
     V("memset", [], T.s[:, 0:3], 0.0)
-    V("memset", [], T.s[:, 275:276], 0.0)
     V("memset", [], T.zb[:], 0.0)
     kf = V("copy", [k], T.pf[:], T.pm[:])
     ze = V("quant", [], T.eq[:, 4 * RG:4 * RG + 160], T.es[:, 4 * RG:4 * RG + 160], T.zt[:])
     if r == 0: k0 = V("memset", [], T.tp[:], 0.0)
 
     for t in range(4): k = V("ts", [ldu], T.ur[:, t:512:4], T.zt[:, 0:128], T.ut[:, t:t + 1], None, A.add)
-    if dn: V("quant", [], T.padq[:, 416:544], T.pads[:, 416:544], T.zt[:, 0:512])
-    qu = V("quant", [k], T.urq[:], T.urs[:], T.ur[:])
     qx, mm = {}, {}
-
-    def score(h, ld):
+    for h, ld in ((0, ldxa), (1, ldxb)):
         c = slice(128 * h, 128 * h + 128)
         qx[h] = V("quant", [ld], T.xq[:, c], T.xs[:, c], T.xt[:, 512 * h:512 * h + 512])
+        if h == 0: qu = V("quant", [k], T.urq[:], T.urs[:], T.ur[:])
         mm[h] = op("t", "mm", [qu, qx[h]], T.sc[:, 512 * h:512 * h + 128], T.urq[:], T.urs[:], T.xq[:, c], T.xs[:, c], True, True)
-    score(0, ldxa)
-    V("memset", [], T.Y[:, L:L + 10], 0.0)
-    V("memset", [], T.Y[:, YW + L:YW + L + 10], 0.0)
-    V("memset", [], T.thr[:, 5:6], 0.0)
-    score(1, ldxb)
-    V("memset", [], T.thr[:, 7:8], 1e9)
-    ko = V("ts", [], T.o7[:], T.zb[:, 0:8], T.pf[:, 1:2], 7.0, A.subtract, A.add)
-    xz = [T.xp[:, (192 if dn else 0) + t:1216 if dn else 1088:68] for t in range(4)] + [T.xp[:, 0:128] if dn else T.xp[:, 1088:1216]]
-    V("memset", [], xz[0], 0.0)
+    if dn: V("quant", [], T.padq[:, 416:544], T.pads[:, 416:544], T.zt[:, 0:512])
+    ko = V("ts", [], T.o7[:], T.zb[:, 0:4], T.pf[:, 1:2], 7.0, A.subtract, A.add)
+    V("memset", [], T.xp[:, 0:128] if dn else T.xp[:, 1088:1216], 0.0)
 
     nb = ([(r - 1, 64, 400)] if up else []) + ([(r + 1, 48, 112)] if r == N - 2 else [])
 
-    def share(q, n, m): return eng[q][n * ne // m:(n + 1) * ne // m]
-
-    def strips(view):
+    def strips(en, view):
         if nb:
-            send([([q], share(q, n, len(nb)), T.sem.halo, view("xq", "xs", src), [view("padq", "pads", dst)]) for n, (q, src, dst) in enumerate(nb)])
+            m = len(en) // len(nb)
+            send([([q], en[n * m:n * m + m], T.sem.halo, view("xq", "xs", src), [view("padq", "pads", dst)]) for n, (q, src, dst) in enumerate(nb)])
     wait("p", [qx[0]])
-    strips(lambda q, s, a: U8(T[q][:, a:a + 16]))
-    hal = ("halo", 2 * (h2 if r in (1, 3) else ne))
+    strips(e0[:h2], lambda q, s, a: U8(T[q][:, a:a + 16]))
+    hal = ("halo", h2 if r in (1, 3) else ne)
 
     S("lin", [kf], T.na[:], T.pf[:, 3:4], -8.0, M128 + 63.5)
     if r == 0: S("lin", [], T.b2[:], T.pf[:, 2:3], 32.0, T.pf[:, 1:2])
@@ -183,139 +174,150 @@ def rank_program(g, core, T, topo):
             a = 64 * ((i + 4) % 16)
             k = S("act", [ldxa, ldxb], T.xp[:, xp0 + 68 * i:xp0 + 68 * i + 64], T.xt[:, a:a + 64], F.Copy)
         return k
-    rows(0, 8)
 
-    V("ts", [mm[0]], T.B[:, 0:32], T.sc[:, 48:80], 1.0 / 32, -1.0 / 32, A.min, A.max)
-    kb = V("ts", [], T.B[:, 32:64], T.sc[:, 48:80], 6.25 / 32, -9.75 / 32, A.min, A.max)
+    def fill(out, n, v): return S("lin", [], out, T.zt[:, 0:n], 0.0, v)
+    rows(0, 7)
 
     def signs(out, a, b, k, deps): return V("ts", deps, out, T.sc[:, a:b], 0.0, k, A.is_gt, A.add)
-    signs(T.s[:, 19:83], 64, 128, -0.5, [])
-    k = signs(T.s[:, 211:275], 0, 64, -0.5, [])
+    if r == 0: k0 = V("turn", [mm[0]], T.BF[:], T.sc[:, 48:80])
+    kb = signs(T.B[:], 48, 80, -0.5, [mm[0]])
+    x = signs(T.s[:, 3:67], 64, 128, -0.5, [])
+    k = signs(T.s[:, 195:259], 0, 64, -0.5, [])
     kb = V("turn", [kb], T.BT[:], T.B[:])
-    sd = S("lin", [k], T.s[:, 3:19], T.s[:, 19:35], 1.0, 0.0)
-    for a, b, c in ((0, 48, 35), (176, 240, 211), (240, 256, 259)): s2 = S("lin", [], T.s2[:, a:b], T.s[:, c:c + b - a], 1.0, 8.0)
-    kX = rows(8, 16)
-    p = signs(T.s[:, 83:211], 512, 640, -0.5, [mm[1]])
-    p2 = signs(T.s2[:, 48:176], 512, 640, 7.5, [])
-    wait("p", [kb])
-    nbr = [q for q in (r - 1, r + 1) if 0 <= q < N]
-    send([([q], share(q, n, len(nbr)), T.sem.bdr, T.BT[:, 31:33], [T.bd[:, 8:10] if q < r else T.bd[:, 0:2]]) for n, q in enumerate(nbr)])
-    strips(lambda q, s, a: T[s][:, a:a + 16])
-    bdr = ("bdr", sum(ne if q in (0, N - 1) else h2 for q in nbr))
-    V("memset", [], xz[1], 0.0)
+    p = signs(T.s[:, 67:195], 512, 640, -0.5, [mm[1]])
+    signs(T.s2[:, 80:208], 512, 640, 7.5, [])
+    p2 = signs(T.s[:, 259:275], 48, 64, -0.5, [])
+    for a, b, c in ((0, 16, 3), (16, 80, 3), (208, 256, 195)): s2 = S("lin", [k if a > 16 else x], T.s2[:, a:b], T.s[:, c:c + b - a], 1.0, 8.0)
+    kX = [rows(7, 9), rows(9, 16)]
 
-    k = V("scan", [p, sd], T.H[:, 0:273], T.s[:, 3:276], T.s[:, 0:273], 0.0, A.add, A.subtract)
-    V("scan", [p2, s2], T.A2[:], T.s[:, 3:259], T.s2[:], 100.0, A.min, A.add)
-    V("tt", [k], T.H[:, 17:273:16], T.s[:, 19:275:16], T.s[:, 20:276:16], A.add)
-    k = V("tt", [], T.H[:, 32:273:16], T.s[:, 33:275:16], T.s[:, 34:275:16], A.add)
-    for j, d in ((1, -1.0), (3, 1.0), (7, -18.0)): V("memset", [], T.Y[:, L + j:2 * YW:YW], -128 * d)
-    k = V("scan", [k], T.T2[:], T.H[:, 17:273], T.A2[:], 100.0, A.min, A.add)
-    for j, d in ((5, 1.0), (9, 34.0)): V("memset", [], T.Y[:, L + j:2 * YW:YW], -128 * d)
-    V("memset", [], xz[2], 0.0)
+    def quant_pad(h):
+        a = (96 if dn else 128) + 152 * h
+        return V("quant", [kX[h], kz], T.padq[:, a:a + 152], T.pads[:, a:a + 152], T.xp[:, 608 * h:608 * h + 608])
+    wait("p", [kb if up else k0])
+    nbr = ([1], [2, 0], [1, 3], [2])[r]
+    if up: send([(nbr, e0[:h2], T.sem["bd%d" % r], T.BT[:, 0:1], [T.bd[:, 8:9] if q < r else T.bd[:, 0:1] for q in nbr])])
+    else: send([(nbr, e0, T.sem.bd0, T.BF[:, 0:1], [T.bf[:, 0:1]])])
+    strips(e0[h2:], lambda q, s, a: T[s][:, a:a + 16])
+    bup, bdn = ("bd%d" % (r - 1), h2 if r > 1 else ne) if up else None, ("bd%d" % (r + 1), h2) if dn else None
+
+    k = V("scan", [p], T.H[:, 0:256], T.s[:, 3:259], T.s[:, 0:256], -8.0, A.add, A.subtract)
+    V("ts", [], T.H[:, 256:257], T.s[:, 257:258], T.s[:, 258:259], -8.0, A.add, A.add)
+    V("scan", [p2, s2], T.A2[:], T.s[:, 19:275], T.s2[:], 100.0, A.min, A.add)
+    V("tt", [k], T.H[:, 1:257:16], T.H[:, 1:257:16], T.s[:, 2:258:16], A.subtract)
+    k = V("tt", [], T.H[:, 16:256:16], T.H[:, 16:256:16], T.s[:, 19:244:16], A.subtract)
+    quant_w()
+    k = V("scan", [k], T.T2[:], T.A2[:], T.H[:, 1:257], -100.0, A.max, A.add)
+    quant_w()
     if up: tt = V("turn", [k], T.TT[:, 32:64], T.T2[:, 0:32])
     if ex_in:
         wait("p", [tt])
         send([([r - 1], e0, T.sem.flg, T.TT[:, 32:33], [T.fl[:, 0:1]])])
     if dn: tt = V("turn", [k], T.TT[:, 0:32], T.T2[:, 224:256])
-    V("ts", [], T.fa[:], T.T2[:], 6.25, None, A.is_gt)
-    k = V("ts", [], T.fb[:], T.T2[:], 9.75, None, A.is_gt)
+    for c in (0, 1): fill(T.Y[:, YW * c + L:YW * c + L + 10:2], 5, 0.0)
+    for j, d in ((1, -1.0), (3, 1.0), (5, 1.0), (7, -18.0), (9, 34.0)): fill(T.Y[:, L + j:2 * YW:YW], 2, -128 * d)
+    if r == 0: fill(T.ik[:], 2, -L * M128 - 128.0 * (PB - 256 + L))
+    fill(T.thr[:, 5:6], 1, 0.0)
+    kS = fill(T.thr[:, 7:8], 1, 1e9)
+    V("ts", [], T.fa[:], T.T2[:], -1.75, None, A.is_gt)
+    if r == 1: y = V("ts", [tt], T.TI[:], T.TT[:, 32:64], 0.3, None, A.mult)
+    k = V("ts", [], T.fb[:], T.T2[:], 1.75, None, A.is_gt)
+    if r > 1: x = V("ts", [bup, tt], T.EL[:, 32:64], T.TT[:, 32:64], T.bd[:, 0:1], -0.9, A.mult, A.is_le)
 
     a, b = (0 if dn else 32), (64 if up else 32)
-    if dn: x = V("ts", [bdr, tt], T.EL[:, 0:32], T.TT[:, 0:32], T.bd[:, 8:9], T.bd[:, 9:10], A.mult, A.is_le)
-    if up: x = V("ts", [bdr, tt], T.EL[:, 32:64], T.TT[:, 32:64], T.bd[:, 0:1], T.bd[:, 1:2], A.mult, A.is_le)
+    if dn: x = V("ts", [bdn, tt], T.EL[:, 0:32], T.TT[:, 0:32], T.bd[:, 8:9], -0.9, A.mult, A.is_le)
+    if r == 1: x = V("ts", [bup, y], T.EL[:, 32:64], T.TI[:], T.bf[:, 0:1], 0.0, A.mult, A.is_lt)
     si = V("scan", [k], T.Si[:], T.fa[:], T.fb[:], 0.0, A.add, A.subtract)
     x = V("turn", [x], T.eb[:, a:b], T.EL[:, a:b])
     x15, x0, c0 = T.eb[:, 16:32], T.eb[:, 32:48], 64 * r
-    V("memset", [], xz[3], 0.0)
-    mp = V("memset", [], xz[4], 0.0)
+    quant_w()
     if r == 0:
         for c in (0, 1): own = V("scan", [x, si, kt], T.inf[:, 32 + c:64:2], x15, T.tp[:, 16 * c:16 * c + 16], T.Si[:, 255:256], A.add, A.add)
     else:
-        if dn: V("scan", [x, si], T.inf[:, c0 + 32:c0 + 64:2], x0, T.zb[:], T.Si[:, 15:16], A.add, A.add)
+        if r == 2: V("scan", [x, si], T.inf[:, c0 + 32:c0 + 64:2], x0, T.zb[:], T.Si[:, 15:16], A.add, A.add)
         own = V("scan", [x, si], T.inf[:, c0 + 33:c0 + 64:2], x0, x15 if dn else T.zb[:], T.Si[:, 255:256], A.add, A.add)
     wait("p", [own])
-    msg = T.inf[:, c0 + (62 if dn else 63):c0 + 64]
+    msg = T.inf[:, c0 + (63 if r % 2 else 62):c0 + 64]
     send([([1, 3, 2] if r == 0 else others[::-1], e0, T.sem["inf%d" % r], msg, [msg] * 3)])
+    if r == 1:
+        wait("p", [V("scan", [], T.inf[:, 80:112:2], x0, T.zb[:], T.Si[:, 15:16], A.add, A.add)])
+        send([(others, e0, T.sem.r01, T.inf[:, 110:111], [T.inf[:, 110:111]] * 3)])
+    r01 = ("r01", ne) if r != 1 else ("vc", cnt["vc"])
     inf = [("inf%d" % q, ne) for q in range(N)]
     flg = ("flg", ne) if ex_out else None
 
     if up: k = V("tt", [], T.fa[:, 0:16], T.fa[:, 0:16], x0, A.add)
     if dn: k = V("tt", [], T.fa[:, 240:256], T.fa[:, 240:256], x15, A.add)
-    if ex_out:
-        x = S("lin", [kb], T.th2[:], T.BT[:, 32:33], 1.0, 3.5 / 32)
-        x = V("ts", [flg, x], T.RB[:], T.BT[:, 0:32], T.fl[:, 0:1], T.th2[:], A.mult, A.is_lt)
+    def below(): return V("ts", [flg], T.RB[:], T.BT[:], T.fl[:, 0:1], 0.9, A.mult, A.is_lt)
+    if r == 1: x = below()
     te = (M128 + 62) / 4 - M128 - 63.5
-    if r == 0: E1 = V("memset", [], T.E1[:], te)
-    if r == 1: E1 = V("ts", [own], T.E1[:], T.inf[:, 127:128], te, None, A.add)
-    if not ex_out: quant_w()
+    if ex_out:
+        for n in (1, 4): E1 = S("lin", [own], T.E1[:, n // 4:n // 4 + 1], T.inf[:, c0 + 63:c0 + 64], float(n * r), n * te)
+    quant_pad(0)
     k = V("scan", [k], T.S[:, 0:256], T.fa[:], T.fb[:], 0.0, A.add, A.subtract)
-    if ex_out: x = V("turn", [x], T.R16[:], T.RB[:])
-    a = 96 if dn else 128
-    pp = V("quant", [kX, mp], T.padq[:, a:a + 304], T.pads[:, a:a + 304], T.xp[:])
+    if r == 0: x = below()
+    if r == 1: x = V("turn", [x], T.R16[:], T.RB[:])
+    pp = quant_pad(1)
+    if r == 0: x = V("turn", [x], T.R16[:], T.RB[:])
     sp = V("copy", [k], T.S[:, 256:272], T.S[:, 15:256:16])
-    if r == 0: sp = V("scan", [x], T.S[:, 272:288], T.R16[:, 0:16], T.zb[:], T.S[:, 255:256], A.add, A.add)
-    if ex_out: sp = V("scan", [x, E1], T.Sl[:], T.R16[:, 0:16], T.zb[:], T.E1[:], A.add, A.add)
-    quant_w((0, 1, 2, 2)[r])
+    if r == 0:
+        quant_w()
+        sp = V("scan", [x], T.S[:, 272:288], T.R16[:, 0:16], T.zb[:], T.S[:, 255:256], A.add, A.add)
+    if ex_out: sp = V("scan", [x, E1], T.Sl[:], T.R16[:, 0:16], T.zb[:], T.E1[:, 0:1], A.add, A.add)
+    quant_w((1, 1, 2, 3)[r])
 
     i0, i1, i2 = T.inf[:, 62:64], T.inf[:, 127:128], T.inf[:, 191:192]
 
     def rounded(c, deps):
         out, a = T.Y[:, YW * c:YW * c + L], T.S[:, 0:L]
         if r == 0: return V("ts", deps, out, a, T.tp[:, 16 - 16 * c:17 - 16 * c], M128 + 128, A.add, A.min)
-        if r == 2: return V("ts", deps, out, a, T.inf[:, 63 - c:64 - c], i1, A.add, A.add)
-        return V("ts", deps, out, a, T.inf[:, 63 - c:64 - c] if r == 1 else T.D[:, 1 - c:2 - c], None, A.add)
+        if r == 1: return V("ts", deps, out, a, T.inf[:, 63 - c:64 - c], None, A.add)
+        return V("ts", deps, out, a, T.inf[:, 63 - c:64 - c] if r == 2 else T.D[:, 1 - c:2 - c], i1, A.add, A.add)
 
-    def start(deps): return V("ts", deps, T.ik[:], T.K[:], -float(L), -128.0 * (PB - 256 + L), A.mult, A.add)
+    def start(deps): return S("lin", deps, T.ik[:], T.K[:], -float(L), -128.0 * (PB - 256 + L))
 
     def count(c, deps):
         a = YW * c
         return V("scan", deps, T.J[:, c:L + 10:2], T.Y[:, a:a + L + 10:2], T.Y[:, a + 1:a + L + 10:2], T.ik[:, 1 - c:2 - c], A.add, A.add)
 
-    def ends(n):
-        if n == 0: return V("scan", inf[:r] + inf[r + 1:], T.thr[:, 0:8:2], T.inf[:, 63:256:64], T.zb[:, 0:4], 0.0, A.add, A.add)
-        if n == 1: return V("ts", [], T.thr[:, 1:2], T.inf[:, 63:64], T.inf[:, 126:127], None, A.add)
-        return V("ts", [], T.thr[:, 3:4], T.inf[:, 63:64], i1, T.inf[:, 190:191], A.add, A.add)
+    def ends(deps, steps):
+        for a, b, c in steps: k = S("lin", deps, T.thr[:, a:a + 1], T.inf[:, c:c + 1], 1.0, T.thr[:, b:b + 1] if b >= 0 else T.inf[:, 63:64])
+        return k
 
     def passed(deps): return V("tt", deps + [kS, ko], T.G[:], T.thr[:].indirect(T.o7[:]), T.nP[:], A.is_le)
     if ex_out:
-        x = V("ts", [E1] + inf[:r], T.Ke[:], T.inf[:, 63:64], T.E1[:], 4.0, A.add, A.mult)
-        if r == 1: k = V("copy", [], T.K[:], i0)
-        V("ts", [sp], T.Ye[:], T.Sl[:], T.inf[:, 63:64], 4.0, A.add, A.mult)
-        rounded(1, [])
-        x = V("ts", [x], T.ike[:], T.Ke[:], -16.0, -128.0 * (PB + 15), A.mult, A.add)
-        k = start([k]) if r == 1 else V("memset", [], T.ik[:], -L * M128 - 128.0 * (PB - 256 + L))
-        y = rounded(0, [])
-        x = V("scan", [x], T.J[:, L - 4:L + 11:2], T.Ye[:, 0:16:2], T.Ye[:, 1:16:2], T.ike[:], A.add, A.add)
-        count(1, [k])
-        quant_w()
-        io = count(0, [x])
-    elif r == 2:
-        k = V("ts", inf[:2], T.K[:], i0, i1, None, A.add)
-        for c in (1, 0): rounded(c, [sp])
-        k = start([k])
-        quant_w()
-        for c in (1, 0): io = count(c, [k])
+        x = S("lin", [E1] + inf[:r], T.Ke[:], T.inf[:, 63:64], 4.0, T.E1[:, 1:2])
+        k = S("lin", [], T.K[:], i0, 1.0, 0.0) if r == 1 else kS
+        x = S("lin", [x], T.ike[:], T.Ke[:], -16.0, -128.0 * (PB + 15))
+        if r == 1: k = start([k])
+        e = V("ts", [sp] + inf[:r], T.Ye[:], T.Sl[:], T.inf[:, 63:64], 4.0, A.add, A.mult)
+        for c in (1, 0): y = rounded(c, [])
+        V("scan", [x, e], T.J[:, L + 24:L + 9:-2], T.Ye[:, 0:16:2], T.Ye[:, 1:16:2], T.ike[:], A.add, A.add)
+        for c in (1, 0): io = count(c, [k, y, kS])
     else:
-        x = V("ts", inf[:3], T.D[:], i0, i1, i2, A.add, A.add)
-        k = V("ts", [], T.K[:], i0, i1, i2, A.add, A.add)
-        quant_w()
-        rounded(1, [sp, x])
+        x = V("ts", [inf[0], inf[2]], T.D[:], i0, i2, None, A.add) if r == 3 else None
+        k = S("lin", inf[:2] + [x], T.K[:], i0 if r == 2 else T.D[:], 1.0, i1)
         k = start([k])
-        y = rounded(0, [])
-        count(1, [k])
-        io = count(0, [y])
+        for c in (1, 0): y = rounded(c, [sp, x] + inf[:2])
+        quant_w()
+        for c in (1, 0): io = count(c, [k, y, kS])
     quant_w()
 
+    k = ends(inf[:r] + inf[r + 1:] + [own], ((2, -1, 127), (0, 5, 63)))
+    th = ends([k], ((4, 2, 191), (3, 2, 190)))
+
     def nio(q): return 11 if r == 1 or (r == 0 and q < 2) else 10
-    def ncs(s, q): return ne if q == (s + 3) % N or s == 0 else h2
+    def order(s):
+        return sorted((q for q in range(N) if q != s), key=lambda q: (topo.die(T.cores[q]) == topo.die(T.cores[s]), (q - s) % 2))
+    def ncs(s, q): return ne if q == order(s)[2] else h2
     def block(t, k, q): return t[32 * k:32 * k + 32, 0:nio(q)]
     def made(q): return T.J[32 * q:32 * q + 32, L:L + nio(q)]
     def spread(q, out): return [S("lin", [io], block(out, k, q), made(q), -1.0 / 128, 256.0) for k in range(4)][-1]
     pls, pqs, pss = [], [], []
-    to = [(r + dq) % N for dq in range(1, N)]
+    to = order(r)
     OF = [T["of%d" % at(q, r)] for q in to]
     z = [[V("ts", [io], block(OF[n], k, to[n]), made(to[n]), -1.0 / 128, 256.0, A.mult, A.add) for k in range(4)][-1] for n in (0, 1)]
     z.append(spread(to[2], T.sp))
+    th = ends([th, r01], ((6, 4, 255), (1, -1, 110)))
     for n, q in enumerate(to):
         i, j, nq = at(q, r), at(r, q), nio(q)
         wd = 168 if nq == 11 else 160
@@ -324,27 +326,22 @@ def rank_program(g, core, T, topo):
         pss.append(S("act", [z[n], pp, hal], T["pks%d" % i][:, 0:16 * nq], T.pads[:].indirect(OF[n][:, 0:nq]), F.Copy))
         pls.append(([q], eng[q][n * h2:n * h2 + h2] if ncs(r, q) == h2 else eng[q], T.sem["cs%d" % j], T["pks%d" % i][:, 0:wd], [T.es[:, RG * r:RG * r + wd]]))
         pqs.append((pq, ([q], eng[q], T.sem["cq%d" % j], U8(T["pkq%d" % i][:, 0:wd]), [U8(T.eq[:, RG * r:RG * r + wd])])))
-    for kind, n in (("q", 0), ("s", 1), ("q", 1), ("s", 2), ("q", 2)):
+    for kind, n in (("q", 0), ("s", 1), ("q", 1), ("q", 2), ("s", 2)):
         wait("p", [pqs[n][0] if kind == "q" else pss[n]])
-        if kind == "q": send([pqs[n][1]])
-        elif n == 2: send(pls[2:])
-        elif r > 0: send(pls[:2])
-        else:
-            for t in pls[:2]: send([t])
+        send([pqs[n][1]] if kind == "q" else pls[2:] if n == 2 else pls[:2])
 
     z = spread(r, T.spo)
-    for n in range(3): th = ends(n)
-    quant_w()
     x = passed([th])
+    quant_w()
+    for c in (0, 64): fd = V("scan", [x], T.Fo[:, c:c + 64], T.G[:], T.W[:, c:c + 64], 0.0, A.mult, A.add)
     no = nio(r)
     y = V("copy", [z], T.ioo[:, 0:no], T.spo[:, 0:no])
     quant_w()
-    x = V("scan", [x], T.Fo[:], T.G[:], T.W[:], 0.0, A.mult, A.add)
     off = T.ioo[:, 0:no]
     pe = V("copy", [y], U32(T.eq[:, RG * r:RG * r + 16 * no]), U32(T.padq[:]).indirect(off))
     pf = S("act", [y], T.es[:, RG * r:RG * r + 16 * no], T.pads[:].indirect(off), F.Copy)
-    fd = V("copy", [x], T.fo[:], T.Fo[:, 7:128:8])
-    quant_w((5, 3, 2, 2)[r])
+    fd = V("copy", [fd], T.fo[:], T.Fo[:, 7:128:8])
+    quant_w()
 
     cq = [("cq%d" % at(q, r), ne) for q in others]
     cs = [("cs%d" % at(q, r), ncs(q, r)) for q in others]
@@ -365,4 +362,4 @@ def rank_program(g, core, T, topo):
     x = S("act", [ms[1]], T.ys[:, 128:256], T.yp[:, 512:640], F.Copy)
     dma("a", "st1", [x], T.y[:, 128:256], T.ys[:, 128:256])
     wait("p", [(k, n) for k, n in cnt.items()])
-    wait("p", [hal, bdr, flg] + inf[:r] + inf[r + 1:])
+    wait("p", [hal, bup, bdn, flg, r01] + inf[:r] + inf[r + 1:])

from concourse.bass import DstId, RemoteDMATransfer
from concourse.mybir import dt, AluOpType, ActivationFunctionType

A = AluOpType
F = ActivationFunctionType
CODE = "float8_e4m3fn_x4"
RG = 176
M128 = 24576.0
YW = 300


def sb(n, d="float32"): return ("sbuf", [128, n], d)


BF, I32, U16 = "bfloat16", "int32", "uint16"
SCRATCH = {
    "ut": sb(8, BF), "ur": sb(512, BF), "xt": sb(1024, BF), "wt": sb(5120, BF), "zt": sb(640, BF), "xp": sb(1216, BF),
    "urq": sb(128, CODE), "urs": sb(128, "uint8"),
    "xq": sb(256, CODE), "xs": sb(256, "uint8"), "padq": sb(544, CODE), "pads": sb(544, "uint8"),
    "wq": sb(1280, CODE), "ws": sb(1280, "uint8"),
    "eq": sb(4 * RG + 160, CODE), "es": sb(4 * RG + 160, "uint8"),
    "xfq": sb(640, CODE), "xfs": sb(640, "uint8"), "ys": sb(256),
    "sc": ("psum", [128, 1024], "float32"), "yp": ("psum", [128, 1024], "float32"),
    "pI": sb(1, I32), "pm": sb(4, I32), "pf": sb(4), "i16": sb(16), "i64": sb(2), "nI": sb(64), "nP": sb(64), "W": sb(128),
    "b2": sb(1), "b3": sb(1), "na": sb(1), "ka": sb(1), "kb": sb(1), "tp": sb(32), "o7": sb(4, U16), "zb": sb(16, BF),
    "s": sb(276, BF), "s2": sb(256, BF), "B": sb(32, BF), "BT": sb(32, BF), "H": sb(274, BF), "A2": sb(256, BF), "T2": sb(256, BF),
    "TT": sb(64, BF), "fa": sb(256, BF), "fb": sb(256, BF), "Si": sb(256, BF), "S": sb(288, BF), "EL": sb(64, BF), "eb": sb(64, BF),
    "bd": sb(16, BF), "BF": sb(32), "bf": sb(4), "TI": sb(32, I32), "fl": sb(8, BF), "inf": sb(256), "E1": sb(2), "ik": sb(2), "ike": sb(1),
    "RB": sb(32, BF), "R16": sb(32, BF), "Sl": sb(16),
    "D": sb(2), "K": sb(2, BF), "Ke": sb(1, BF), "Y": sb(2 * YW, BF), "Ye": sb(16, BF), "J": sb(320, BF),
    "thr": sb(8), "G": sb(64), "Fo": sb(128), "fo": sb(16, U16), "ioo": sb(12, U16), "spo": sb(12), "sp": sb(12),
}
for _i in range(3):
    SCRATCH["of%d" % _i] = sb(12, U16)
    SCRATCH["pkq%d" % _i] = sb(RG, CODE)
    SCRATCH["pks%d" % _i] = sb(RG, "uint8")
SEMAPHORES = ["vc", "ac", "tc", "pc", "ldu", "ldxa", "ldxb", "ldw0", "ldw1", "ldw2", "ldw3", "ldw4", "halo", "bd0", "bd1", "bd2", "bd3", "inf0", "inf1", "inf2", "inf3",
              "flg", "r01", "cq0", "cq1", "cq2", "cs0", "cs1", "cs2", "sent", "st0", "st1"]


def rank_program(g, core, T, topo):
    r = T.rank_of(core)
    if r is None:
        return
    N = len(T.cores)
    others = [q for q in range(N) if q != r]
    Q = {"v": g.vector, "a": g.scalar, "t": g.tensor, "p": g, "s": g.sync}
    cnt, seen = {"sent": 0}, {}

    def wait(qn, deps):
        for d in deps:
            if d is not None and seen.get((qn, d[0]), 0) < d[1]:
                Q[qn].wait_ge(T.sem[d[0]], d[1])
                seen[(qn, d[0])] = d[1]

    def tok(sem, inst, n):
        inst.then_inc(T.sem[sem], n)
        cnt[sem] = cnt.get(sem, 0) + n
        return (sem, cnt[sem])

    def op(qn, name, deps, *args):
        wait(qn, deps)
        q = Q[qn]
        if name == "memset": i = q.memset(*args)
        elif name == "tt": i = q.tensor_tensor(*args)
        elif name == "ts": i = q.tensor_scalar(*args)
        elif name == "copy": i = q.tensor_copy(*args)
        elif name == "scan": i = q.tensor_tensor_scan(*args)
        elif name == "turn": i = q.transpose(*args)
        elif name == "quant": i = q.quantize_mx(*args)
        elif name == "act": i = q.activation(*args)
        elif name == "lin": i = q.activation(args[0], args[1], F.Identity, bias=args[3], scale=args[2])
        elif name == "mm": i = q.matmul_mx(*args)
        elif name == "iota": i = q.iota(*args)
        else: i = q.iota(*args, allow_small_or_imprecise_dtypes=True)
        return tok(qn + "c", i, 1)

    def V(name, deps, *args): return op("v", name, deps, *args)
    def S(name, deps, *args): return op("a", name, deps, *args)

    def dma(qn, sem, deps, out, in_):
        wait(qn, deps)
        return tok(sem, Q[qn].dma_start(out, in_), 16)

    def U8(v): return v.bitcast(dt.uint8)
    def U32(v): return v.bitcast(dt.uint32)
    def bits(en): return sum(1 << e for e in en)

    def dest(q):
        rid, pid, _ = topo.addr(T.cores[q])
        return DstId(rid=rid, pnc=pid)

    def send(trs):
        g.remote_dma_fused([RemoteDMATransfer(dst_ids=[dest(q) for q in qs], dma_engine_mask=bits(en), remote_sem=sem, srcs=[src], dsts=dsts)
                            for qs, en, sem, src, dsts in trs], local_sem=T.sem.sent)
        cnt["sent"] += sum(len(t[1]) for t in trs)

    def at(q, me): return q if q < me else q - 1
    eng = {q: topo.engines(core, T.cores[q]) for q in others}
    ne = min(len(eng[q]) for q in others)
    e0 = eng[others[0]]
    h2 = ne // 2

    up, dn = r > 0, r < N - 1
    ex_out, ex_in = r in (0, 1), r in (1, 2)
    PB = 128 if dn else 129
    L = 288 if r == 0 else 272
    ldw, qw = {}, {}

    def load_w(k, deps): ldw[k] = dma("s", "ldw%d" % k, deps, T.wt[:, 1024 * k:1024 * k + 1024], T.w[:, 1024 * k:1024 * k + 1024])

    def quant_w(m=1):
        for n in range(len(qw), min(10, len(qw) + m)):
            qw[n] = V("quant", [ldw[n // 2]], T.wq[:, 128 * n:128 * n + 128], T.ws[:, 128 * n:128 * n + 128], T.wt[:, 512 * n:512 * n + 512])
    ldu = dma("a", "ldu", [], T.ut[:], T.u[:, 0:8])
    dma("s", "ldxa", [], T.xt[:, 256:512], T.x[:, 0:256])
    ldxa = dma("a", "ldxa", [], T.xt[:, 0:256], T.x[:, 768:1024])
    ldxb = dma("s", "ldxb", [], T.xt[:, 512:1024], T.x[:, 256:768])
    for k in range(5): load_w(k, [])
    kp = op("p", "iota", [], T.pI[:], [[0, 1]], 0, 1)
    op("p", "iotaf", [], T.i16[:], [[0, 8], [16, 2]], 0, 0)
    if r == 0: op("p", "iotaf", [], T.i64[:], [[64, 2]], -64, 0)
    op("p", "iotaf", [], T.W[:], [[0, 64], [-RG, 2]], RG, 0)
    kg = op("p", "iotaf", [], T.nI[:], [[64, 8], [0, 8]], 8 * r, 0)
    for t in range(4): kz = op("p", "iotaf", [], T.xp[:, (192 if dn else 0) + t:1216 if dn else 1088:68], [[0, 16]], 0, 0)
    mz = V("memset", [], T.zt[:], 0.0)
    V("ts", [kp], T.pm[:, 3:4], T.pI[:], 5, None, A.logical_shift_right)
    V("ts", [], T.pm[:, 0:1], T.pI[:], 15, None, A.bitwise_and)
    V("ts", [], T.pm[:, 1:2], T.pI[:], 7, None, A.bitwise_and)
    k = V("ts", [], T.pm[:, 2:3], T.pI[:], 3, 1, A.logical_shift_right, A.bitwise_and)
    V("memset", [], T.s[:, 0:3], 0.0)
    V("memset", [], T.zb[:], 0.0)
    kf = V("copy", [k], T.pf[:], T.pm[:])
    ze = V("quant", [], T.eq[:, 4 * RG:4 * RG + 160], T.es[:, 4 * RG:4 * RG + 160], T.zt[:])
    if r == 0: k0 = V("memset", [], T.tp[:], 0.0)

    for t in range(4): k = V("ts", [ldu], T.ur[:, t:512:4], T.zt[:, 0:128], T.ut[:, t:t + 1], None, A.add)
    qx, mm = {}, {}
    for h, ld in ((0, ldxa), (1, ldxb)):
        c = slice(128 * h, 128 * h + 128)
        qx[h] = V("quant", [ld], T.xq[:, c], T.xs[:, c], T.xt[:, 512 * h:512 * h + 512])
        if h == 0: qu = V("quant", [k], T.urq[:], T.urs[:], T.ur[:])
        mm[h] = op("t", "mm", [qu, qx[h]], T.sc[:, 512 * h:512 * h + 128], T.urq[:], T.urs[:], T.xq[:, c], T.xs[:, c], True, True)
    if dn: V("quant", [], T.padq[:, 416:544], T.pads[:, 416:544], T.zt[:, 0:512])
    ko = V("ts", [], T.o7[:], T.zb[:, 0:4], T.pf[:, 1:2], 7.0, A.subtract, A.add)
    V("memset", [], T.xp[:, 0:128] if dn else T.xp[:, 1088:1216], 0.0)

    nb = ([(r - 1, 64, 400)] if up else []) + ([(r + 1, 48, 112)] if r == N - 2 else [])

    def strips(en, view):
        if nb:
            m = len(en) // len(nb)
            send([([q], en[n * m:n * m + m], T.sem.halo, view("xq", "xs", src), [view("padq", "pads", dst)]) for n, (q, src, dst) in enumerate(nb)])
    wait("p", [qx[0]])
    strips(e0[:h2], lambda q, s, a: U8(T[q][:, a:a + 16]))
    hal = ("halo", h2 if r in (1, 3) else ne)

    S("lin", [kf], T.na[:], T.pf[:, 3:4], -8.0, M128 + 63.5)
    if r == 0: S("lin", [], T.b2[:], T.pf[:, 2:3], 32.0, T.pf[:, 1:2])
    S("lin", [], T.ka[:], T.pf[:, 2:3], 8.0, RG - 64.0)
    k = S("lin", [], T.kb[:], T.pf[:, 2:3], -8.0, 64.0)
    S("lin", [kg], T.W[:, 7:128:8], T.i16[:], 1.0, T.pf[:, 0:1])
    if r == 0: kt = S("lin", [k], T.b3[:], T.b2[:], -1.0, T.na[:])
    S("lin", [k], T.nP[:], T.nI[:], 1.0, T.na[:])
    for j in (3, 5):
        plain = j == 5 and r >= 2
        S("lin", [], T.W[:, 64 + j:128:8], T.i16[:, 0:8], 0.0 if plain else 1.0, float(RG) if plain else T.ka[:])
        kS = S("lin", [], T.W[:, 65 + j:128:8], T.i16[:, 0:8], 0.0 if plain else -1.0, 0.0 if plain else T.kb[:])
    if r == 0: kt = S("lin", [kt, k0], T.tp[:, 0:32:16], T.i64[:], 1.0, T.b3[:])
    xp0 = 128 if dn else 4

    def rows(lo, hi):
        for i in range(lo, hi):
            a = 64 * ((i + 4) % 16)
            k = S("act", [ldxa, ldxb], T.xp[:, xp0 + 68 * i:xp0 + 68 * i + 64], T.xt[:, a:a + 64], F.Copy)
        return k

    def fill(out, n, v): return S("lin", [], out, T.zt[:, 0:n], 0.0, v)
    rows(0, 7)

    def signs(out, a, b, k, deps): return V("ts", deps, out, T.sc[:, a:b], 0.0, k, A.is_gt, A.add)
    if r == 0: k0 = V("turn", [mm[0]], T.BF[:], T.sc[:, 48:80])
    kb = signs(T.B[:], 48, 80, -0.5, [mm[0]])
    x = signs(T.s[:, 3:67], 64, 128, -0.5, [])
    k = signs(T.s[:, 195:259], 0, 64, -0.5, [])
    kb = V("turn", [kb], T.BT[:], T.B[:])
    p = signs(T.s[:, 67:195], 512, 640, -0.5, [mm[1]])
    signs(T.s2[:, 80:208], 512, 640, 7.5, [])
    p2 = signs(T.s[:, 259:275], 48, 64, -0.5, [])
    for a, b, c in ((0, 16, 3), (16, 80, 3), (208, 256, 195)): s2 = S("lin", [k if a > 16 else x], T.s2[:, a:b], T.s[:, c:c + b - a], 1.0, 8.0)
    kX = [rows(7, 9), rows(9, 16)]

    def quant_pad(h):
        a = (96 if dn else 128) + 152 * h
        return V("quant", [kX[h], kz], T.padq[:, a:a + 152], T.pads[:, a:a + 152], T.xp[:, 608 * h:608 * h + 608])
    wait("p", [kb if up else k0])
    nbr = ([1], [2, 0], [1, 3], [2])[r]
    if up: send([(nbr, e0[:h2], T.sem["bd%d" % r], T.BT[:, 0:1], [T.bd[:, 8:9] if q < r else T.bd[:, 0:1] for q in nbr])])
    else: send([(nbr, e0, T.sem.bd0, T.BF[:, 0:1], [T.bf[:, 0:1]])])
    strips(e0[h2:], lambda q, s, a: T[s][:, a:a + 16])
    bup, bdn = ("bd%d" % (r - 1), h2 if r > 1 else ne) if up else None, ("bd%d" % (r + 1), h2) if dn else None

    k = V("scan", [p], T.H[:, 0:256], T.s[:, 3:259], T.s[:, 0:256], -8.0, A.add, A.subtract)
    V("ts", [], T.H[:, 256:257], T.s[:, 257:258], T.s[:, 258:259], -8.0, A.add, A.add)
    V("scan", [p2, s2], T.A2[:], T.s[:, 19:275], T.s2[:], 100.0, A.min, A.add)
    V("tt", [k], T.H[:, 1:257:16], T.H[:, 1:257:16], T.s[:, 2:258:16], A.subtract)
    k = V("tt", [], T.H[:, 16:256:16], T.H[:, 16:256:16], T.s[:, 19:244:16], A.subtract)
    quant_w()
    k = V("scan", [k], T.T2[:], T.A2[:], T.H[:, 1:257], -100.0, A.max, A.add)
    quant_w()
    if up: tt = V("turn", [k], T.TT[:, 32:64], T.T2[:, 0:32])
    if ex_in:
        wait("p", [tt])
        send([([r - 1], e0, T.sem.flg, T.TT[:, 32:33], [T.fl[:, 0:1]])])
    if dn: tt = V("turn", [k], T.TT[:, 0:32], T.T2[:, 224:256])
    for c in (0, 1): fill(T.Y[:, YW * c + L:YW * c + L + 10:2], 5, 0.0)
    for j, d in ((1, -1.0), (3, 1.0), (5, 1.0), (7, -18.0), (9, 34.0)): fill(T.Y[:, L + j:2 * YW:YW], 2, -128 * d)
    if r == 0: fill(T.ik[:], 2, -L * M128 - 128.0 * (PB - 256 + L))
    fill(T.thr[:, 5:6], 1, 0.0)
    kS = fill(T.thr[:, 7:8], 1, 1e9)
    V("ts", [], T.fa[:], T.T2[:], -1.75, None, A.is_gt)
    if r == 1: y = V("ts", [tt], T.TI[:], T.TT[:, 32:64], 0.3, None, A.mult)
    k = V("ts", [], T.fb[:], T.T2[:], 1.75, None, A.is_gt)
    if r > 1: x = V("ts", [bup, tt], T.EL[:, 32:64], T.TT[:, 32:64], T.bd[:, 0:1], -0.9, A.mult, A.is_le)

    a, b = (0 if dn else 32), (64 if up else 32)
    if dn: x = V("ts", [bdn, tt], T.EL[:, 0:32], T.TT[:, 0:32], T.bd[:, 8:9], -0.9, A.mult, A.is_le)
    if r == 1: x = V("ts", [bup, y], T.EL[:, 32:64], T.TI[:], T.bf[:, 0:1], 0.0, A.mult, A.is_lt)
    si = V("scan", [k], T.Si[:], T.fa[:], T.fb[:], 0.0, A.add, A.subtract)
    x = V("turn", [x], T.eb[:, a:b], T.EL[:, a:b])
    x15, x0, c0 = T.eb[:, 16:32], T.eb[:, 32:48], 64 * r
    quant_w()
    if r == 0:
        for c in (0, 1): own = V("scan", [x, si, kt], T.inf[:, 32 + c:64:2], x15, T.tp[:, 16 * c:16 * c + 16], T.Si[:, 255:256], A.add, A.add)
    else:
        if r == 2: V("scan", [x, si], T.inf[:, c0 + 32:c0 + 64:2], x0, T.zb[:], T.Si[:, 15:16], A.add, A.add)
        own = V("scan", [x, si], T.inf[:, c0 + 33:c0 + 64:2], x0, x15 if dn else T.zb[:], T.Si[:, 255:256], A.add, A.add)
    wait("p", [own])
    msg = T.inf[:, c0 + (63 if r % 2 else 62):c0 + 64]
    send([([1, 3, 2] if r == 0 else others[::-1], e0, T.sem["inf%d" % r], msg, [msg] * 3)])
    if r == 1:
        wait("p", [V("scan", [], T.inf[:, 80:112:2], x0, T.zb[:], T.Si[:, 15:16], A.add, A.add)])
        send([(others, e0, T.sem.r01, T.inf[:, 110:111], [T.inf[:, 110:111]] * 3)])
    r01 = ("r01", ne) if r != 1 else ("vc", cnt["vc"])
    inf = [("inf%d" % q, ne) for q in range(N)]
    flg = ("flg", ne) if ex_out else None

    if up: k = V("tt", [], T.fa[:, 0:16], T.fa[:, 0:16], x0, A.add)
    if dn: k = V("tt", [], T.fa[:, 240:256], T.fa[:, 240:256], x15, A.add)
    def below(): return V("ts", [flg], T.RB[:], T.BT[:], T.fl[:, 0:1], 0.9, A.mult, A.is_lt)
    if r == 1: x = below()
    te = (M128 + 62) / 4 - M128 - 63.5
    if ex_out:
        for n in (1, 4): E1 = S("lin", [own], T.E1[:, n // 4:n // 4 + 1], T.inf[:, c0 + 63:c0 + 64], float(n * r), n * te)
    quant_pad(0)
    k = V("scan", [k], T.S[:, 0:256], T.fa[:], T.fb[:], 0.0, A.add, A.subtract)
    if r == 0: x = below()
    if r == 1: x = V("turn", [x], T.R16[:], T.RB[:])
    pp = quant_pad(1)
    if r == 0: x = V("turn", [x], T.R16[:], T.RB[:])
    sp = V("copy", [k], T.S[:, 256:272], T.S[:, 15:256:16])
    if r == 0:
        quant_w()
        sp = V("scan", [x], T.S[:, 272:288], T.R16[:, 0:16], T.zb[:], T.S[:, 255:256], A.add, A.add)
    if ex_out: sp = V("scan", [x, E1], T.Sl[:], T.R16[:, 0:16], T.zb[:], T.E1[:, 0:1], A.add, A.add)
    quant_w((1, 1, 2, 3)[r])

    i0, i1, i2 = T.inf[:, 62:64], T.inf[:, 127:128], T.inf[:, 191:192]

    def rounded(c, deps):
        out, a = T.Y[:, YW * c:YW * c + L], T.S[:, 0:L]
        if r == 0: return V("ts", deps, out, a, T.tp[:, 16 - 16 * c:17 - 16 * c], M128 + 128, A.add, A.min)
        if r == 1: return V("ts", deps, out, a, T.inf[:, 63 - c:64 - c], None, A.add)
        return V("ts", deps, out, a, T.inf[:, 63 - c:64 - c] if r == 2 else T.D[:, 1 - c:2 - c], i1, A.add, A.add)

    def start(deps): return S("lin", deps, T.ik[:], T.K[:], -float(L), -128.0 * (PB - 256 + L))

    def count(c, deps):
        a = YW * c
        return V("scan", deps, T.J[:, c:L + 10:2], T.Y[:, a:a + L + 10:2], T.Y[:, a + 1:a + L + 10:2], T.ik[:, 1 - c:2 - c], A.add, A.add)

    def ends(deps, steps):
        for a, b, c in steps: k = S("lin", deps, T.thr[:, a:a + 1], T.inf[:, c:c + 1], 1.0, T.thr[:, b:b + 1] if b >= 0 else T.inf[:, 63:64])
        return k

    def passed(deps): return V("tt", deps + [kS, ko], T.G[:], T.thr[:].indirect(T.o7[:]), T.nP[:], A.is_le)
    if ex_out:
        x = S("lin", [E1] + inf[:r], T.Ke[:], T.inf[:, 63:64], 4.0, T.E1[:, 1:2])
        k = S("lin", [], T.K[:], i0, 1.0, 0.0) if r == 1 else kS
        x = S("lin", [x], T.ike[:], T.Ke[:], -16.0, -128.0 * (PB + 15))
        if r == 1: k = start([k])
        e = V("ts", [sp] + inf[:r], T.Ye[:], T.Sl[:], T.inf[:, 63:64], 4.0, A.add, A.mult)
        for c in (1, 0): y = rounded(c, [])
        V("scan", [x, e], T.J[:, L + 24:L + 9:-2], T.Ye[:, 0:16:2], T.Ye[:, 1:16:2], T.ike[:], A.add, A.add)
        for c in (1, 0): io = count(c, [k, y, kS])
    else:
        x = V("ts", [inf[0], inf[2]], T.D[:], i0, i2, None, A.add) if r == 3 else None
        k = S("lin", inf[:2] + [x], T.K[:], i0 if r == 2 else T.D[:], 1.0, i1)
        k = start([k])
        for c in (1, 0): y = rounded(c, [sp, x] + inf[:2])
        quant_w()
        for c in (1, 0): io = count(c, [k, y, kS])
    quant_w()

    k = ends(inf[:r] + inf[r + 1:] + [own], ((2, -1, 127), (0, 5, 63)))
    th = ends([k], ((4, 2, 191), (3, 2, 190)))

    def nio(q): return 11 if r == 1 or (r == 0 and q < 2) else 10
    def order(s):
        return sorted((q for q in range(N) if q != s), key=lambda q: (topo.die(T.cores[q]) == topo.die(T.cores[s]), (q - s) % 2))
    def ncs(s, q): return ne if q == order(s)[2] else h2
    def block(t, k, q): return t[32 * k:32 * k + 32, 0:nio(q)]
    def made(q): return T.J[32 * q:32 * q + 32, L:L + nio(q)]
    def spread(q, out): return [S("lin", [io], block(out, k, q), made(q), -1.0 / 128, 256.0) for k in range(4)][-1]
    pls, pqs, pss = [], [], []
    to = order(r)
    OF = [T["of%d" % at(q, r)] for q in to]
    z = [[V("ts", [io], block(OF[n], k, to[n]), made(to[n]), -1.0 / 128, 256.0, A.mult, A.add) for k in range(4)][-1] for n in (0, 1)]
    z.append(spread(to[2], T.sp))
    th = ends([th, r01], ((6, 4, 255), (1, -1, 110)))
    for n, q in enumerate(to):
        i, j, nq = at(q, r), at(r, q), nio(q)
        wd = 168 if nq == 11 else 160
        pq = V("copy", [z[n], pp, hal], U32(T["pkq%d" % i][:, 0:16 * nq]), U32(T.padq[:]).indirect(OF[n][:, 0:nq]))
        if n == 0: z[2] = V("copy", [z[2]], OF[2][:, 0:nio(to[2])], T.sp[:, 0:nio(to[2])])
        pss.append(S("act", [z[n], pp, hal], T["pks%d" % i][:, 0:16 * nq], T.pads[:].indirect(OF[n][:, 0:nq]), F.Copy))
        pls.append(([q], eng[q][n * h2:n * h2 + h2] if ncs(r, q) == h2 else eng[q], T.sem["cs%d" % j], T["pks%d" % i][:, 0:wd], [T.es[:, RG * r:RG * r + wd]]))
        pqs.append((pq, ([q], eng[q], T.sem["cq%d" % j], U8(T["pkq%d" % i][:, 0:wd]), [U8(T.eq[:, RG * r:RG * r + wd])])))
    for kind, n in (("q", 0), ("s", 1), ("q", 1), ("q", 2), ("s", 2)):
        wait("p", [pqs[n][0] if kind == "q" else pss[n]])
        send([pqs[n][1]] if kind == "q" else pls[2:] if n == 2 else pls[:2])

    z = spread(r, T.spo)
    x = passed([th])
    quant_w()
    for c in (0, 64): fd = V("scan", [x], T.Fo[:, c:c + 64], T.G[:], T.W[:, c:c + 64], 0.0, A.mult, A.add)
    no = nio(r)
    y = V("copy", [z], T.ioo[:, 0:no], T.spo[:, 0:no])
    quant_w()
    off = T.ioo[:, 0:no]
    pe = V("copy", [y], U32(T.eq[:, RG * r:RG * r + 16 * no]), U32(T.padq[:]).indirect(off))
    pf = S("act", [y], T.es[:, RG * r:RG * r + 16 * no], T.pads[:].indirect(off), F.Copy)
    fd = V("copy", [fd], T.fo[:], T.Fo[:, 7:128:8])
    quant_w()

    cq = [("cq%d" % at(q, r), ne) for q in others]
    cs = [("cs%d" % at(q, r), ncs(q, r)) for q in others]
    for n, k in enumerate((1, 3, 4, 0, 2)):
        lo, hi = 128 * n, 128 * n + 128
        s = slice(32 * k, 32 * k + 4 * RG + 32)
        off = T.fo[:, 8:16] if k == 3 else T.fo[:, 0:8]
        a = V("copy", [pe, fd] + cq, U32(T.xfq[:, lo:hi]), U32(T.eq[:, s]).indirect(off))
        quant_w()
        b = S("act", [pf, fd, ze] + cs, T.xfs[:, lo:hi], T.es[:, s].indirect(off), F.Copy)
        ms = []
        for o in range(2):
            w = 128 * (2 * n + o)
            ms.append(op("t", "mm", [a, b, qw[2 * n + o]], T.yp[:, 512 * o:512 * o + 128],
                         T.wq[:, w:w + 128], T.ws[:, w:w + 128], T.xfq[:, lo:hi], T.xfs[:, lo:hi], n == 0, n == 4))
    x = V("copy", [ms[0]], T.ys[:, 0:128], T.yp[:, 0:128])
    dma("s", "st0", [x], T.y[:, 0:128], T.ys[:, 0:128])
    x = S("act", [ms[1]], T.ys[:, 128:256], T.yp[:, 512:640], F.Copy)
    dma("a", "st1", [x], T.y[:, 128:256], T.ys[:, 128:256])
    wait("p", [(k, n) for k, n in cnt.items()])
    wait("p", [hal, bup, bdn, flg, r01] + inf[:r] + inf[r + 1:])
